import numpy as np
import ml_dtypes


def mxq(x, axis, fmt="e4m3"):
    dtype, down = {"e4m3": (ml_dtypes.float8_e4m3fn, 7), "e5m2": (ml_dtypes.float8_e5m2, 14)}[fmt]
    v = np.moveaxis(np.asarray(x, np.float32).astype(ml_dtypes.bfloat16).astype(np.float64), axis, -1)
    blocks = v.reshape(v.shape[:-1] + (-1, 32))
    amax = np.abs(blocks).max(-1, keepdims=True)
    byte = np.maximum(np.where(amax > 0, np.frexp(amax)[1] - 1 + 127, 0) - down, 1)
    scale = np.exp2(byte - 127.0)
    codes = (blocks / scale).astype(np.float32).astype(dtype).astype(np.float64)
    return np.moveaxis((codes * scale).reshape(v.shape), -1, axis)


WIDE = False


def mx_kscale(k):
    if not WIDE:
        return np.ones(k)
    levels = np.array([10, -10, 5, -5, 0])
    if k % 512:
        return np.exp2(np.random.permutation(np.resize(levels, k // 32))).repeat(32)
    a = np.empty((k // 512, 16))
    for p in range(k // 512):
        a[p, :8] = np.random.permutation(np.resize(levels, 8))
        for g in range(8):
            far = levels[np.abs(levels - a[p, g]) >= 10]
            a[p, g + 8] = far[np.random.randint(len(far))]
    return np.exp2(a.ravel()).repeat(32)


def f64(x):
    return np.asarray(x).astype(np.float64)


def striped(idx):
    return np.tile(np.asarray(idx).reshape(-1, 16).T, (8, 1)).astype(np.uint16)


def unstriped(offs):
    return offs[:16].T.reshape(-1).astype(np.int64)


E2M1 = np.array([0.0, 0.5, 1.0, 1.5, 2.0, 3.0, 4.0, 6.0, -0.0, -0.5, -1.0, -1.5, -2.0, -3.0, -4.0, -6.0])


def pack_weight(w, fmt):
    k, n = w.shape
    w = f64(np.asarray(w, np.float32).astype(ml_dtypes.bfloat16)).reshape(k // 32, 32, n)
    amax = np.abs(w).max(1)
    if fmt == "e4m3":
        byte = np.frexp(amax)[1] - 1 + 127 - 7
    else:
        mant, ex = np.frexp(amax / 6.0)
        byte = np.where(mant > 0.5, ex, ex - 1) + 127
    byte = np.clip(np.where(amax > 0, byte, 1), 1, 254)
    scaled = (w * np.exp2(127.0 - byte)[:, None, :]).reshape(k, n).astype(np.float32)
    by_word = np.ascontiguousarray(scaled.reshape(k // 512, 128, 4, n).transpose(0, 1, 3, 2))
    if fmt == "e4m3":
        words = by_word.astype(ml_dtypes.float8_e4m3fn).view(np.uint8)
    else:
        c = by_word.astype(ml_dtypes.float4_e2m1fn).view(np.uint8) & 0xF
        words = (c[..., 0::2] | (c[..., 1::2] << 4)).reshape(k // 512, 128, 2 * n)
    return np.ascontiguousarray(words), np.ascontiguousarray(byte.astype(np.uint8).reshape(k // 512, 16, n))


def unpack_weight(words, scales, fmt):
    g, _, n = scales.shape
    words = np.ascontiguousarray(words).reshape(g, 128, n, -1)
    if fmt == "e4m3":
        vals = words.view(ml_dtypes.float8_e4m3fn).astype(np.float64)
    else:
        nib = np.empty((g, 128, n, 4), np.uint8)
        nib[..., 0::2] = words & 0xF
        nib[..., 1::2] = words >> 4
        vals = E2M1[nib]
    vals = vals * np.repeat(np.exp2(scales.astype(np.float64) - 127.0), 8, axis=1)[..., None]
    return vals.transpose(0, 1, 3, 2).reshape(g * 512, n)


B, N, T, D, DV, NQ = 1, 2048, 4096, 512, 128, 128
PAGE = 512
CAP = 2.0


def setup_inputs():
    n = np.random.standard_normal
    pages = np.random.permutation(T // PAGE)[:B * N // PAGE]
    idx = (pages[:, None] * PAGE + np.arange(PAGE)[None, :]).reshape(-1)
    s = mx_kscale(D)[:, None]
    u = np.ones(T)
    u[idx] = mx_kscale(B * N)
    r = np.random.uniform(0.5, 2.0, T)
    qp = [pack_weight(x, "e4m3") for x in n((B, D, NQ)) * s * (1.00 / np.sqrt(D))]
    k = n((D, T)) / s
    v = n((DV, T)) / (u * r)
    kp = pack_weight(k, "e4m3")
    vp = pack_weight(v.T, "e4m3")
    return {
        "q_words": np.stack([x[0] for x in qp]),
        "q_scales": np.stack([x[1] for x in qp]),
        "k_words": kp[0],
        "k_scales": kp[1],
        "v_words": vp[0],
        "v_scales": vp[1],
        "vs": np.tile(u * r, (128, 1)).astype(np.float32),
        "og": n((B, NQ, DV)).astype(np.float32),
        "offs": striped(idx),
        "voffs": striped((pages[:, None] * DV + np.arange(DV)[None, :]).reshape(-1)),
    }


def reference(q_words, q_scales, k_words, k_scales, v_words, v_scales, vs, og, offs, voffs):
    idx = unstriped(offs)
    k = unpack_weight(k_words, k_scales, "e4m3")
    v = unpack_weight(v_words, v_scales, "e4m3")
    v = v.reshape(T // 512, 512, DV)[unstriped(voffs)[::DV] // DV].reshape(B, N, DV)
    pick = lambda x: x[:, idx].reshape(x.shape[0], B, N).transpose(1, 0, 2)
    q = np.stack([unpack_weight(q_words[b], q_scales[b], "e4m3") for b in range(B)])
    score = q.transpose(0, 2, 1) @ pick(k)
    score = CAP * np.tanh(score / CAP)
    m = score.max(-1, keepdims=True)
    p = np.exp(score - m)
    total = p.sum(-1, keepdims=True)
    w = p * pick(f64(vs))[:, :1, :]
    y = mxq(w, 2, "e4m3") @ v
    y = y / total
    y = y / (1.0 + np.exp(-f64(og)))
    return y

@@ -1,0 +1,212 @@
+from contextlib import ExitStack
+
+import concourse.mybir as mybir
+from concourse.masks import make_identity
+
+F32 = mybir.dt.float32
+BF16 = mybir.dt.bfloat16
+I32 = mybir.dt.int32
+U32 = mybir.dt.uint32
+U16 = mybir.dt.uint16
+U8 = mybir.dt.uint8
+FP8X4 = mybir.dt.float8_e4m3fn_x4
+ACT = mybir.ActivationFunctionType
+ALU = mybir.AluOpType
+AXIS = mybir.AxisListType
+
+P = 128
+NQ, SLOTS, POOL, D, DV = 128, 2048, 4096, 512, 128
+PAGE = 512
+PAGES = SLOTS // PAGE
+POOL_PAGES = POOL // PAGE
+CAP = 2.0
+LIST_COLS = PAGE // 16
+
+FLOPS = 2 * NQ * SLOTS * D + 2 * NQ * SLOTS * DV
+
+
+def tile_attend_pkv8q_soft_cap_gate_kernel(
+    tc, q_words, q_scales, k_words, k_scales, v_words, v_scales, vs, og, offs, voffs, out
+):
+    nc = tc.nc
+    with ExitStack() as ctx:
+        held = ctx.enter_context(tc.tile_pool(name="held", bufs=1))
+        reused = ctx.enter_context(tc.tile_pool(name="reused", bufs=1))
+        ring = ctx.enter_context(tc.tile_pool(name="ring", bufs=PAGES))
+        score_banks = ctx.enter_context(tc.psum_pool(name="score_banks", bufs=PAGES))
+        turn_banks = ctx.enter_context(tc.psum_pool(name="turn_banks", bufs=3))
+        out_bank = ctx.enter_context(tc.psum_pool(name="out_bank", bufs=1))
+
+        slot_list = held.tile([P, SLOTS // 16], U16, name="slot_list")
+        nc.sync.dma_start(slot_list[:], offs)
+        column_list = held.tile([P, PAGES * DV // 16], U16, name="column_list")
+        nc.sync.dma_start(column_list[:], voffs)
+
+        query_codes = held.tile([P, NQ], I32, name="query_codes", align_bytes=64)
+        nc.sync.dma_start(query_codes[:], q_words[0, 0].rearrange("p q r -> p (q r)").bitcast(I32))
+
+        key_scale_pool = held.tile([P, POOL // 4], I32, name="key_scale_pool")
+        nc.vector.memset(key_scale_pool[:], 0)
+        key_scale_rows = k_scales[0].bitcast(I32).rearrange("(a r) t -> r a t", r=4)
+        for r in range(4):
+            nc.sync.dma_start(key_scale_pool[r:P:32, :], key_scale_rows[r])
+
+        key_pool = held.tile([P, POOL], I32, name="key_pool")
+        nc.sync.dma_start(key_pool[:], k_words[0].rearrange("p t r -> p (t r)").bitcast(I32))
+        vs_pool = reused.tile([P, POOL], F32, name="vs_pool", offset=0)
+        nc.sync.dma_start(vs_pool[:], vs)
+
+        value_scale_pool = held.tile([P, POOL_PAGES * DV // 4], I32, name="value_scale_pool")
+        nc.vector.memset(value_scale_pool[:], 0)
+        value_scale_rows = v_scales.bitcast(I32).rearrange("u (a r) e -> r a u e", r=4)
+        for r in range(4):
+            nc.sync.dma_start(
+                value_scale_pool[r:P:32, :].rearrange("a (u e) -> a u e", u=POOL_PAGES), value_scale_rows[r]
+            )
+        value_pool = held.tile([P, POOL_PAGES * DV], I32, name="value_pool")
+        nc.sync.dma_start(
+            value_pool[:].rearrange("p (u e) -> p u e", u=POOL_PAGES),
+            v_words.rearrange("u p e r -> p u (e r)").bitcast(I32),
+        )
+
+        query_scales = held.tile([P, NQ // 4], I32, name="query_scales", align_bytes=64)
+        nc.gpsimd.memset(query_scales[:], 0)
+        query_scale_rows = q_scales[0, 0].bitcast(I32).rearrange("(a r) q -> r a q", r=4)
+        for r in range(4):
+            nc.gpsimd.dma_start(query_scales[r:P:32, :], query_scale_rows[r])
+        gate_logits = held.tile([P, DV], F32, name="gate_logits")
+        nc.gpsimd.dma_start(gate_logits[:], og[0])
+
+        identity = held.tile([P, P], F32, name="identity")
+        make_identity(nc, identity[:])
+
+        key_scales = held.tile([P, SLOTS], U8, name="key_scales", align_bytes=64)
+        nc.vector.tensor_copy(key_scales[:], key_scale_pool[:].bitcast(U8).indirect(slot_list[:]))
+
+        def page_slots(g):
+            return slice(g * PAGE, (g + 1) * PAGE)
+
+        def page_list(g):
+            return slot_list[:, g * LIST_COLS : (g + 1) * LIST_COLS]
+
+        key_codes = held.tile([P, SLOTS], U32, name="key_codes", tag="keys_then_exp", align_bytes=64)
+        for g in range(PAGES):
+            nc.vector.tensor_copy(key_codes[:, page_slots(g)], key_pool[:].bitcast(U32).indirect(page_list(g)))
+
+        capped = held.tile([P, SLOTS + PAGES - 1], F32, name="capped")
+        for g in range(PAGES):
+            scores = score_banks.tile([P, PAGE], F32, name="scores")
+            nc.tensor.matmul_mx(
+                scores[:],
+                lhsT=query_codes[:].bitcast(FP8X4),
+                lhsT_scale=query_scales[:].bitcast(U8),
+                rhs=key_codes[:, page_slots(g)].bitcast(FP8X4),
+                rhs_scale=key_scales[:, page_slots(g)],
+                start=True,
+                stop=True,
+            )
+            nc.scalar.activation(capped[:, page_slots(g)], scores[:], ACT.Tanh, scale=1.0 / CAP)
+
+        for g in range(PAGES - 1):
+            nc.vector.tensor_reduce(capped[:, SLOTS + g : SLOTS + g + 1], capped[:, page_slots(g)], AXIS.X, ALU.max)
+        row_max = held.tile([P, 1], F32, name="row_max")
+        nc.vector.tensor_reduce(row_max[:], capped[:, (PAGES - 1) * PAGE :], AXIS.X, ALU.max)
+        exp_neg_max = held.tile([P, 1], F32, name="exp_neg_max")
+        nc.scalar.activation(exp_neg_max[:], row_max[:], ACT.Exp, scale=-CAP)
+
+        exp_capped = held.tile([P, SLOTS], F32, name="exp_capped", tag="keys_then_exp", align_bytes=64)
+        page_sums = held.tile([P, PAGES], F32, name="page_sums")
+        for g in range(PAGES):
+            nc.scalar.activation(
+                exp_capped[:, page_slots(g)],
+                capped[:, page_slots(g)],
+                ACT.Exp,
+                scale=CAP,
+                accum_out=page_sums[:, g : g + 1],
+            )
+
+        scaled = {}
+        grouped = {}
+        weights = {}
+        codes = {}
+
+        def times_vs(g):
+            scaled[g] = ring.tile([P, PAGE], F32, name="scaled")
+            nc.vector.tensor_tensor(
+                scaled[g][:], vs_pool[:].indirect(page_list(g)), exp_capped[:, page_slots(g)], ALU.mult
+            )
+
+        def round_weights(g, on_vector):
+            weights[g] = ring.tile([P, 2, P, 2], BF16, name="weights")
+            source = scaled[g][:].rearrange("q (s u e) -> q u s e", u=2, e=2)
+            if on_vector:
+                nc.vector.tensor_scalar(weights[g][:], source, exp_neg_max[:], None, ALU.mult)
+            else:
+                nc.scalar.activation(weights[g][:], source, ACT.Copy, scale=exp_neg_max[:])
+
+        def turn(g):
+            words = weights[g][:].rearrange("q u s e -> q (u s e)").bitcast(F32)
+            turned = turn_banks.tile([P, 2, NQ], F32, name="turned")
+            for u in range(2):
+                nc.tensor.transpose(turned[:, u, :], words[:, u * P : (u + 1) * P], identity[:])
+            grouped[g] = ring.tile([P, NQ * 4], BF16, name="grouped", align_bytes=64)
+            nc.scalar.copy(
+                grouped[g][:].bitcast(F32).rearrange("s (q u) -> s q u", u=2), turned[:].rearrange("s u q -> s q u")
+            )
+
+        def quantise(g):
+            weight_codes = ring.tile([P, NQ], U32, name="weight_codes", align_bytes=64)
+            weight_scales = ring.tile([P, NQ], U8, name="weight_scales", align_bytes=64)
+            nc.vector.quantize_mx(out=weight_codes[:].bitcast(FP8X4), scales=weight_scales[:], in_=grouped[g][:])
+            codes[g] = (weight_codes, weight_scales)
+
+        times_vs(0)
+        times_vs(1)
+        round_weights(0, True)
+        turn(0)
+        times_vs(2)
+        times_vs(3)
+        round_weights(1, False)
+        turn(1)
+        quantise(0)
+        round_weights(3, True)
+        round_weights(2, False)
+        turn(2)
+        turn(3)
+
+        value_scales = reused.tile([P, PAGES * DV], U8, name="value_scales", align_bytes=64, offset=PAGES * DV * 4)
+        nc.vector.tensor_copy(value_scales[:], value_scale_pool[:].bitcast(U8).indirect(column_list[:]))
+        value_codes = reused.tile([P, PAGES * DV], U32, name="value_codes", align_bytes=64, offset=0)
+        nc.vector.tensor_copy(value_codes[:], value_pool[:].bitcast(U32).indirect(column_list[:]))
+
+        gate_tanh = held.tile([P, DV], F32, name="gate_tanh")
+        nc.scalar.activation(gate_tanh[:], gate_logits[:], ACT.Tanh, scale=0.5)
+
+        scaled_sums = held.tile([P, PAGES], F32, name="scaled_sums")
+        nc.vector.tensor_scalar(scaled_sums[:], page_sums[:], exp_neg_max[:], 2.0, ALU.mult, ALU.mult)
+        row_sum = held.tile([P, 1], F32, name="row_sum")
+        nc.vector.tensor_reduce(row_sum[:], scaled_sums[:], AXIS.X, ALU.add)
+        inverse_sum = held.tile([P, 1], F32, name="inverse_sum")
+        nc.vector.reciprocal(inverse_sum[:], row_sum[:])
+        factor = held.tile([P, DV], F32, name="factor")
+        nc.vector.tensor_scalar(factor[:], gate_tanh[:], 1.0, inverse_sum[:], ALU.add, ALU.mult)
+
+        for g in range(1, PAGES):
+            quantise(g)
+
+        sums = out_bank.tile([P, DV], F32, name="sums")
+        for g in range(PAGES):
+            columns = slice(g * DV, (g + 1) * DV)
+            nc.tensor.matmul_mx(
+                sums[:],
+                lhsT=codes[g][0][:].bitcast(FP8X4),
+                lhsT_scale=codes[g][1][:],
+                rhs=value_codes[:, columns].bitcast(FP8X4),
+                rhs_scale=value_scales[:, columns],
+                start=(g == 0),
+                stop=(g == PAGES - 1),
+            )
+
+        result = held.tile([P, DV], F32, name="result")
+        nc.vector.tensor_tensor(result[:], sums[:], factor[:], ALU.mult)
+        nc.sync.dma_start(out[0], result[:])

@@ -21,6 +21,7 @@ PAGES = SLOTS // PAGE
 POOL_PAGES = POOL // PAGE
 CAP = 2.0
 LIST_COLS = PAGE // 16
+EARLY_KEYS = POOL // 4
 
 FLOPS = 2 * NQ * SLOTS * D + 2 * NQ * SLOTS * DV
 
@@ -39,11 +40,13 @@ def tile_attend_pkv8q_soft_cap_gate_kernel(
 
         slot_list = held.tile([P, SLOTS // 16], U16, name="slot_list")
         nc.sync.dma_start(slot_list[:], offs)
+
+        key_pool = held.tile([P, POOL], I32, name="key_pool")
+        key_words = k_words[0].rearrange("p t r -> p (t r)").bitcast(I32)
+        nc.sync.dma_start(key_pool[:, :EARLY_KEYS], key_words[:, :EARLY_KEYS])
+
         column_list = held.tile([P, PAGES * DV // 16], U16, name="column_list")
         nc.sync.dma_start(column_list[:], voffs)
-
-        query_codes = held.tile([P, NQ], I32, name="query_codes", align_bytes=64)
-        nc.sync.dma_start(query_codes[:], q_words[0, 0].rearrange("p q r -> p (q r)").bitcast(I32))
 
         key_scale_pool = held.tile([P, POOL // 4], I32, name="key_scale_pool")
         nc.vector.memset(key_scale_pool[:], 0)
@@ -51,8 +54,18 @@ def tile_attend_pkv8q_soft_cap_gate_kernel(
         for r in range(4):
             nc.sync.dma_start(key_scale_pool[r:P:32, :], key_scale_rows[r])
 
-        key_pool = held.tile([P, POOL], I32, name="key_pool")
-        nc.sync.dma_start(key_pool[:], k_words[0].rearrange("p t r -> p (t r)").bitcast(I32))
+        nc.sync.dma_start(key_pool[:, EARLY_KEYS:], key_words[:, EARLY_KEYS:])
+
+        query_codes = held.tile([P, NQ], I32, name="query_codes", align_bytes=64)
+        nc.sync.dma_start(query_codes[:], q_words[0, 0].rearrange("p q r -> p (q r)").bitcast(I32))
+        query_scales = held.tile([P, NQ // 4], I32, name="query_scales", align_bytes=64)
+        nc.vector.memset(query_scales[:], 0)
+        query_scale_rows = q_scales[0, 0].bitcast(I32).rearrange("(a r) q -> r a q", r=4)
+        for r in range(4):
+            nc.sync.dma_start(query_scales[r:P:32, :], query_scale_rows[r])
+        gate_logits = held.tile([P, DV], F32, name="gate_logits")
+        nc.sync.dma_start(gate_logits[:], og[0])
+
         vs_pool = reused.tile([P, POOL], F32, name="vs_pool", offset=0)
         nc.sync.dma_start(vs_pool[:], vs)
 
@@ -69,16 +82,13 @@ def tile_attend_pkv8q_soft_cap_gate_kernel(
             v_words.rearrange("u p e r -> p u (e r)").bitcast(I32),
         )
 
-        query_scales = held.tile([P, NQ // 4], I32, name="query_scales", align_bytes=64)
-        nc.gpsimd.memset(query_scales[:], 0)
-        query_scale_rows = q_scales[0, 0].bitcast(I32).rearrange("(a r) q -> r a q", r=4)
-        for r in range(4):
-            nc.gpsimd.dma_start(query_scales[r:P:32, :], query_scale_rows[r])
-        gate_logits = held.tile([P, DV], F32, name="gate_logits")
-        nc.gpsimd.dma_start(gate_logits[:], og[0])
-
         identity = held.tile([P, P], F32, name="identity")
         make_identity(nc, identity[:])
+
+        gate_tanh = held.tile([P, DV], F32, name="gate_tanh")
+        nc.scalar.activation(gate_tanh[:], gate_logits[:], ACT.Tanh, scale=0.5)
+        gate = held.tile([P, DV], F32, name="gate")
+        nc.scalar.activation(gate[:], gate_tanh[:], ACT.Copy, scale=0.5, bias=0.5)
 
         key_scales = held.tile([P, SLOTS], U8, name="key_scales", align_bytes=64)
         nc.vector.tensor_copy(key_scales[:], key_scale_pool[:].bitcast(U8).indirect(slot_list[:]))
@@ -160,39 +170,26 @@ def tile_attend_pkv8q_soft_cap_gate_kernel(
             nc.vector.quantize_mx(out=weight_codes[:].bitcast(FP8X4), scales=weight_scales[:], in_=grouped[g][:])
             codes[g] = (weight_codes, weight_scales)
 
-        times_vs(0)
-        times_vs(1)
-        round_weights(0, True)
-        turn(0)
-        times_vs(2)
-        times_vs(3)
-        round_weights(1, False)
-        turn(1)
-        quantise(0)
-        round_weights(3, True)
-        round_weights(2, False)
-        turn(2)
-        turn(3)
+        for g in range(PAGES):
+            times_vs(g)
+        for g in range(PAGES):
+            round_weights(g, g >= PAGES // 2)
+        for g in range(PAGES):
+            turn(g)
 
         value_scales = reused.tile([P, PAGES * DV], U8, name="value_scales", align_bytes=64, offset=PAGES * DV * 4)
         nc.vector.tensor_copy(value_scales[:], value_scale_pool[:].bitcast(U8).indirect(column_list[:]))
         value_codes = reused.tile([P, PAGES * DV], U32, name="value_codes", align_bytes=64, offset=0)
         nc.vector.tensor_copy(value_codes[:], value_pool[:].bitcast(U32).indirect(column_list[:]))
 
-        gate_tanh = held.tile([P, DV], F32, name="gate_tanh")
-        nc.scalar.activation(gate_tanh[:], gate_logits[:], ACT.Tanh, scale=0.5)
+        for g in range(PAGES):
+            quantise(g)
 
         scaled_sums = held.tile([P, PAGES], F32, name="scaled_sums")
-        nc.vector.tensor_scalar(scaled_sums[:], page_sums[:], exp_neg_max[:], 2.0, ALU.mult, ALU.mult)
         row_sum = held.tile([P, 1], F32, name="row_sum")
-        nc.vector.tensor_reduce(row_sum[:], scaled_sums[:], AXIS.X, ALU.add)
+        nc.scalar.activation(scaled_sums[:], page_sums[:], ACT.Copy, scale=exp_neg_max[:], accum_out=row_sum[:])
         inverse_sum = held.tile([P, 1], F32, name="inverse_sum")
         nc.vector.reciprocal(inverse_sum[:], row_sum[:])
-        factor = held.tile([P, DV], F32, name="factor")
-        nc.vector.tensor_scalar(factor[:], gate_tanh[:], 1.0, inverse_sum[:], ALU.add, ALU.mult)
-
-        for g in range(1, PAGES):
-            quantise(g)
 
         sums = out_bank.tile([P, DV], F32, name="sums")
         for g in range(PAGES):
@@ -208,5 +205,5 @@ def tile_attend_pkv8q_soft_cap_gate_kernel(
             )
 
         result = held.tile([P, DV], F32, name="result")
-        nc.vector.tensor_tensor(result[:], sums[:], factor[:], ALU.mult)
+        nc.vector.scalar_tensor_tensor(result[:], sums[:], inverse_sum[:], gate[:], ALU.mult, ALU.mult)
         nc.sync.dma_start(out[0], result[:])

@@ -22,6 +22,8 @@ POOL_PAGES = POOL // PAGE
 CAP = 2.0
 LIST_COLS = PAGE // 16
 EARLY_KEYS = POOL // 4
+VS_LOADED = POOL // 2
+VS_PER_PARTITION = (POOL - VS_LOADED) // P
 
 FLOPS = 2 * NQ * SLOTS * D + 2 * NQ * SLOTS * DV
 
@@ -41,12 +43,12 @@ def tile_attend_pkv8q_soft_cap_gate_kernel(
         slot_list = held.tile([P, SLOTS // 16], U16, name="slot_list")
         nc.sync.dma_start(slot_list[:], offs)
 
+        vs_row = held.tile([P, VS_PER_PARTITION], F32, name="vs_row")
+        nc.scalar.dma_start(vs_row[:], vs[0, VS_LOADED:].rearrange("(p j) -> p j", p=P))
+
         key_pool = held.tile([P, POOL], I32, name="key_pool")
         key_words = k_words[0].rearrange("p t r -> p (t r)").bitcast(I32)
         nc.sync.dma_start(key_pool[:, :EARLY_KEYS], key_words[:, :EARLY_KEYS])
-
-        column_list = held.tile([P, PAGES * DV // 16], U16, name="column_list")
-        nc.sync.dma_start(column_list[:], voffs)
 
         key_scale_pool = held.tile([P, POOL // 4], I32, name="key_scale_pool")
         nc.vector.memset(key_scale_pool[:], 0)
@@ -56,6 +58,9 @@ def tile_attend_pkv8q_soft_cap_gate_kernel(
 
         nc.sync.dma_start(key_pool[:, EARLY_KEYS:], key_words[:, EARLY_KEYS:])
 
+        gate_logits = held.tile([P, DV], F32, name="gate_logits")
+        nc.sync.dma_start(gate_logits[:], og[0])
+
         query_codes = held.tile([P, NQ], I32, name="query_codes", align_bytes=64)
         nc.sync.dma_start(query_codes[:], q_words[0, 0].rearrange("p q r -> p (q r)").bitcast(I32))
         query_scales = held.tile([P, NQ // 4], I32, name="query_scales", align_bytes=64)
@@ -63,11 +68,12 @@ def tile_attend_pkv8q_soft_cap_gate_kernel(
         query_scale_rows = q_scales[0, 0].bitcast(I32).rearrange("(a r) q -> r a q", r=4)
         for r in range(4):
             nc.sync.dma_start(query_scales[r:P:32, :], query_scale_rows[r])
-        gate_logits = held.tile([P, DV], F32, name="gate_logits")
-        nc.sync.dma_start(gate_logits[:], og[0])
 
         vs_pool = reused.tile([P, POOL], F32, name="vs_pool", offset=0)
-        nc.sync.dma_start(vs_pool[:], vs)
+        nc.sync.dma_start(vs_pool[:, :VS_LOADED], vs[:, :VS_LOADED])
+
+        column_list = held.tile([P, PAGES * DV // 16], U16, name="column_list")
+        nc.sync.dma_start(column_list[:], voffs)
 
         value_scale_pool = held.tile([P, POOL_PAGES * DV // 4], I32, name="value_scale_pool")
         nc.vector.memset(value_scale_pool[:], 0)
@@ -84,6 +90,14 @@ def tile_attend_pkv8q_soft_cap_gate_kernel(
 
         identity = held.tile([P, P], F32, name="identity")
         make_identity(nc, identity[:])
+
+        spread = vs_pool[:, VS_LOADED:].rearrange("r (p j) -> r p j", p=P)
+        for first in range(0, VS_PER_PARTITION, 4):
+            turned = turn_banks.tile([P, 4, P], F32, name="turned")
+            for j in range(4):
+                column = vs_row[:, first + j : first + j + 1].to_broadcast([P, P])
+                nc.tensor.transpose(turned[:, j, :], column, identity[:])
+            nc.scalar.activation(spread[:, :, first : first + 4], turned[:].rearrange("r j p -> r p j"), ACT.Copy)
 
         gate_tanh = held.tile([P, DV], F32, name="gate_tanh")
         nc.scalar.activation(gate_tanh[:], gate_logits[:], ACT.Tanh, scale=0.5)
@@ -185,10 +199,10 @@ def tile_attend_pkv8q_soft_cap_gate_kernel(
         for g in range(PAGES):
             quantise(g)
 
-        scaled_sums = held.tile([P, PAGES], F32, name="scaled_sums")
+        scaled_sums = ring.tile([P, PAGES], F32, name="scaled")
         row_sum = held.tile([P, 1], F32, name="row_sum")
         nc.scalar.activation(scaled_sums[:], page_sums[:], ACT.Copy, scale=exp_neg_max[:], accum_out=row_sum[:])
-        inverse_sum = held.tile([P, 1], F32, name="inverse_sum")
+        inverse_sum = reused.tile([P, 1], F32, name="inverse_sum", offset=PAGES * DV * 5)
         nc.vector.reciprocal(inverse_sum[:], row_sum[:])
 
         sums = out_bank.tile([P, DV], F32, name="sums")

@@ -21,7 +21,7 @@ PAGES = SLOTS // PAGE
 POOL_PAGES = POOL // PAGE
 CAP = 2.0
 LIST_COLS = PAGE // 16
-EARLY_KEYS = POOL // 4
+EARLY_KEYS = POOL // 8
 VS_LOADED = POOL // 2
 VS_PER_PARTITION = (POOL - VS_LOADED) // P
 
@@ -44,14 +44,15 @@ def tile_attend_pkv8q_soft_cap_gate_kernel(
         nc.sync.dma_start(slot_list[:], offs)
 
         vs_row = held.tile([P, VS_PER_PARTITION], F32, name="vs_row")
-        nc.scalar.dma_start(vs_row[:], vs[0, VS_LOADED:].rearrange("(p j) -> p j", p=P))
+        nc.sync.dma_start(vs_row[:], vs[0, VS_LOADED:].rearrange("(p j) -> p j", p=P))
 
         key_pool = held.tile([P, POOL], I32, name="key_pool")
         key_words = k_words[0].rearrange("p t r -> p (t r)").bitcast(I32)
         nc.sync.dma_start(key_pool[:, :EARLY_KEYS], key_words[:, :EARLY_KEYS])
 
         key_scale_pool = held.tile([P, POOL // 4], I32, name="key_scale_pool")
-        nc.vector.memset(key_scale_pool[:], 0)
+        nc.gpsimd.memset(key_scale_pool[:, : POOL // 8], 0)
+        nc.vector.memset(key_scale_pool[:, POOL // 8 :], 0)
         key_scale_rows = k_scales[0].bitcast(I32).rearrange("(a r) t -> r a t", r=4)
         for r in range(4):
             nc.sync.dma_start(key_scale_pool[r:P:32, :], key_scale_rows[r])
@@ -194,9 +195,11 @@ def tile_attend_pkv8q_soft_cap_gate_kernel(
         value_scales = reused.tile([P, PAGES * DV], U8, name="value_scales", align_bytes=64, offset=PAGES * DV * 4)
         nc.vector.tensor_copy(value_scales[:], value_scale_pool[:].bitcast(U8).indirect(column_list[:]))
         value_codes = reused.tile([P, PAGES * DV], U32, name="value_codes", align_bytes=64, offset=0)
-        nc.vector.tensor_copy(value_codes[:], value_pool[:].bitcast(U32).indirect(column_list[:]))
-
         for g in range(PAGES):
+            page_columns = column_list[:, g * DV // 16 : (g + 1) * DV // 16]
+            nc.vector.tensor_copy(
+                value_codes[:, g * DV : (g + 1) * DV], value_pool[:].bitcast(U32).indirect(page_columns)
+            )
             quantise(g)
 
         scaled_sums = ring.tile([P, PAGES], F32, name="scaled")

@@ -21,7 +21,7 @@ PAGES = SLOTS // PAGE
 POOL_PAGES = POOL // PAGE
 CAP = 2.0
 LIST_COLS = PAGE // 16
-EARLY_KEYS = POOL // 8
+EARLY_KEYS = POOL // 16
 VS_LOADED = POOL // 2
 VS_PER_PARTITION = (POOL - VS_LOADED) // P
 
@@ -35,6 +35,7 @@ def tile_attend_pkv8q_soft_cap_gate_kernel(
     with ExitStack() as ctx:
         held = ctx.enter_context(tc.tile_pool(name="held", bufs=1))
         reused = ctx.enter_context(tc.tile_pool(name="reused", bufs=1))
+        stage = ctx.enter_context(tc.tile_pool(name="stage", bufs=1))
         ring = ctx.enter_context(tc.tile_pool(name="ring", bufs=PAGES))
         score_banks = ctx.enter_context(tc.psum_pool(name="score_banks", bufs=PAGES))
         turn_banks = ctx.enter_context(tc.psum_pool(name="turn_banks", bufs=3))
@@ -139,11 +140,16 @@ def tile_attend_pkv8q_soft_cap_gate_kernel(
         exp_neg_max = held.tile([P, 1], F32, name="exp_neg_max")
         nc.scalar.activation(exp_neg_max[:], row_max[:], ACT.Exp, scale=-CAP)
 
-        exp_capped = held.tile([P, SLOTS], F32, name="exp_capped", tag="keys_then_exp", align_bytes=64)
+        first_exp = held.tile([P, PAGE], F32, name="first_exp")
+        later_exp = held.tile([P, SLOTS], F32, name="later_exp", tag="keys_then_exp", align_bytes=64)
+
+        def exp_capped(first, width):
+            return first_exp[:, first : first + width] if first < PAGE else later_exp[:, first : first + width]
+
         page_sums = held.tile([P, PAGES], F32, name="page_sums")
         for g in range(PAGES):
             nc.scalar.activation(
-                exp_capped[:, page_slots(g)],
+                exp_capped(g * PAGE, PAGE),
                 capped[:, page_slots(g)],
                 ACT.Exp,
                 scale=CAP,
@@ -155,26 +161,38 @@ def tile_attend_pkv8q_soft_cap_gate_kernel(
         weights = {}
         codes = {}
 
-        def times_vs(g):
-            scaled[g] = ring.tile([P, PAGE], F32, name="scaled")
-            nc.vector.tensor_tensor(
-                scaled[g][:], vs_pool[:].indirect(page_list(g)), exp_capped[:, page_slots(g)], ALU.mult
-            )
+        def times_vs(g, parts):
+            scaled[g] = stage.tile([P, PAGE], F32, name="scaled%d" % g, align_bytes=64, offset=g * PAGE * 4)
+            width = PAGE // parts
+            for first in range(0, PAGE, width):
+                slot = g * PAGE + first
+                nc.vector.tensor_tensor(
+                    scaled[g][:, first : first + width],
+                    vs_pool[:].indirect(slot_list[:, slot // 16 : (slot + width) // 16]),
+                    exp_capped(slot, width),
+                    ALU.mult,
+                )
 
-        def round_weights(g, on_vector):
+        def round_weights(g, parts):
             weights[g] = ring.tile([P, 2, P, 2], BF16, name="weights")
             source = scaled[g][:].rearrange("q (s u e) -> q u s e", u=2, e=2)
-            if on_vector:
-                nc.vector.tensor_scalar(weights[g][:], source, exp_neg_max[:], None, ALU.mult)
-            else:
-                nc.scalar.activation(weights[g][:], source, ACT.Copy, scale=exp_neg_max[:])
+            width = P // parts
+            for first in range(0, P, width):
+                nc.scalar.activation(
+                    weights[g][:, :, first : first + width, :],
+                    source[:, :, first : first + width, :],
+                    ACT.Copy,
+                    scale=exp_neg_max[:],
+                )
 
         def turn(g):
             words = weights[g][:].rearrange("q u s e -> q (u s e)").bitcast(F32)
             turned = turn_banks.tile([P, 2, NQ], F32, name="turned")
             for u in range(2):
                 nc.tensor.transpose(turned[:, u, :], words[:, u * P : (u + 1) * P], identity[:])
-            grouped[g] = ring.tile([P, NQ * 4], BF16, name="grouped", align_bytes=64)
+            grouped[g] = stage.tile(
+                [P, NQ * 4], BF16, name="grouped%d" % g, align_bytes=64, offset=(g + 1) * PAGE * 4
+            )
             nc.scalar.copy(
                 grouped[g][:].bitcast(F32).rearrange("s (q u) -> s q u", u=2), turned[:].rearrange("s u q -> s q u")
             )
@@ -186,23 +204,20 @@ def tile_attend_pkv8q_soft_cap_gate_kernel(
             codes[g] = (weight_codes, weight_scales)
 
         for g in range(PAGES):
-            times_vs(g)
+            times_vs(g, 2 if g == PAGES - 1 else 1)
         for g in range(PAGES):
-            round_weights(g, g >= PAGES // 2)
+            round_weights(g, 2 if g == PAGES - 1 else 1)
         for g in range(PAGES):
             turn(g)
 
         value_scales = reused.tile([P, PAGES * DV], U8, name="value_scales", align_bytes=64, offset=PAGES * DV * 4)
         nc.vector.tensor_copy(value_scales[:], value_scale_pool[:].bitcast(U8).indirect(column_list[:]))
         value_codes = reused.tile([P, PAGES * DV], U32, name="value_codes", align_bytes=64, offset=0)
+        nc.vector.tensor_copy(value_codes[:], value_pool[:].bitcast(U32).indirect(column_list[:]))
         for g in range(PAGES):
-            page_columns = column_list[:, g * DV // 16 : (g + 1) * DV // 16]
-            nc.vector.tensor_copy(
-                value_codes[:, g * DV : (g + 1) * DV], value_pool[:].bitcast(U32).indirect(page_columns)
-            )
             quantise(g)
 
-        scaled_sums = ring.tile([P, PAGES], F32, name="scaled")
+        scaled_sums = stage.tile([P, PAGES], F32, name="scaled_sums", align_bytes=64, offset=0)
         row_sum = held.tile([P, 1], F32, name="row_sum")
         nc.scalar.activation(scaled_sums[:], page_sums[:], ACT.Copy, scale=exp_neg_max[:], accum_out=row_sum[:])
         inverse_sum = reused.tile([P, 1], F32, name="inverse_sum", offset=PAGES * DV * 5)

@@ -173,17 +173,13 @@ def tile_attend_pkv8q_soft_cap_gate_kernel(
                     ALU.mult,
                 )
 
-        def round_weights(g, parts):
+        def round_weights(g, on_vector):
             weights[g] = ring.tile([P, 2, P, 2], BF16, name="weights")
             source = scaled[g][:].rearrange("q (s u e) -> q u s e", u=2, e=2)
-            width = P // parts
-            for first in range(0, P, width):
-                nc.scalar.activation(
-                    weights[g][:, :, first : first + width, :],
-                    source[:, :, first : first + width, :],
-                    ACT.Copy,
-                    scale=exp_neg_max[:],
-                )
+            if on_vector:
+                nc.vector.tensor_scalar(weights[g][:], source, exp_neg_max[:], None, ALU.mult)
+            else:
+                nc.scalar.activation(weights[g][:], source, ACT.Copy, scale=exp_neg_max[:])
 
         def turn(g):
             words = weights[g][:].rearrange("q u s e -> q (u s e)").bitcast(F32)
@@ -191,7 +187,7 @@ def tile_attend_pkv8q_soft_cap_gate_kernel(
             for u in range(2):
                 nc.tensor.transpose(turned[:, u, :], words[:, u * P : (u + 1) * P], identity[:])
             grouped[g] = stage.tile(
-                [P, NQ * 4], BF16, name="grouped%d" % g, align_bytes=64, offset=(g + 1) * PAGE * 4
+                [P, NQ * 4], BF16, name="grouped%d" % g, align_bytes=64, offset=(1 if g == 0 else PAGES + g) * PAGE * 4
             )
             nc.scalar.copy(
                 grouped[g][:].bitcast(F32).rearrange("s (q u) -> s q u", u=2), turned[:].rearrange("s u q -> s q u")
@@ -204,9 +200,9 @@ def tile_attend_pkv8q_soft_cap_gate_kernel(
             codes[g] = (weight_codes, weight_scales)
 
         for g in range(PAGES):
-            times_vs(g, 2 if g == PAGES - 1 else 1)
+            times_vs(g, 1)
         for g in range(PAGES):
-            round_weights(g, 2 if g == PAGES - 1 else 1)
+            round_weights(g, g >= PAGES // 2)
         for g in range(PAGES):
             turn(g)
 

@@ -21,9 +21,8 @@ PAGES = SLOTS // PAGE
 POOL_PAGES = POOL // PAGE
 CAP = 2.0
 LIST_COLS = PAGE // 16
-EARLY_KEYS = POOL // 16
-VS_LOADED = POOL // 2
-VS_PER_PARTITION = (POOL - VS_LOADED) // P
+EARLY_KEYS = POOL // 8
+LATE_KEYS = 3 * POOL // 8
 
 FLOPS = 2 * NQ * SLOTS * D + 2 * NQ * SLOTS * DV
 
@@ -44,70 +43,70 @@ def tile_attend_pkv8q_soft_cap_gate_kernel(
         slot_list = held.tile([P, SLOTS // 16], U16, name="slot_list")
         nc.sync.dma_start(slot_list[:], offs)
 
-        vs_row = held.tile([P, VS_PER_PARTITION], F32, name="vs_row")
-        nc.sync.dma_start(vs_row[:], vs[0, VS_LOADED:].rearrange("(p j) -> p j", p=P))
-
         key_pool = held.tile([P, POOL], I32, name="key_pool")
         key_words = k_words[0].rearrange("p t r -> p (t r)").bitcast(I32)
         nc.sync.dma_start(key_pool[:, :EARLY_KEYS], key_words[:, :EARLY_KEYS])
 
-        key_scale_pool = held.tile([P, POOL // 4], I32, name="key_scale_pool")
-        nc.gpsimd.memset(key_scale_pool[:, : POOL // 8], 0)
-        nc.vector.memset(key_scale_pool[:, POOL // 8 :], 0)
-        key_scale_rows = k_scales[0].bitcast(I32).rearrange("(a r) t -> r a t", r=4)
-        for r in range(4):
-            nc.sync.dma_start(key_scale_pool[r:P:32, :], key_scale_rows[r])
+        key_scale_pool = reused.tile([P, POOL // 4], I32, name="key_scale_pool", align_bytes=64, offset=POOL * 4 - 64)
+        nc.vector.memset(key_scale_pool[:], 0)
+        nc.sync.dma_start(key_scale_pool[0:P:8, :], k_scales[0].bitcast(I32))
 
-        nc.sync.dma_start(key_pool[:, EARLY_KEYS:], key_words[:, EARLY_KEYS:])
+        column_list = held.tile([P, PAGES * DV // 16], U16, name="column_list")
+        nc.sync.dma_start(column_list[:], voffs)
+        value_scale_pool = held.tile([P, POOL_PAGES * DV // 4], I32, name="value_scale_pool")
+        nc.vector.memset(value_scale_pool[:], 0)
+        nc.sync.dma_start(
+            value_scale_pool[0:P:8, :].rearrange("f (u e) -> f u e", u=POOL_PAGES),
+            v_scales.bitcast(I32).rearrange("u f e -> f u e"),
+        )
 
-        gate_logits = held.tile([P, DV], F32, name="gate_logits")
-        nc.sync.dma_start(gate_logits[:], og[0])
+        nc.sync.dma_start(key_pool[:, EARLY_KEYS:LATE_KEYS], key_words[:, EARLY_KEYS:LATE_KEYS])
 
-        query_codes = held.tile([P, NQ], I32, name="query_codes", align_bytes=64)
-        nc.sync.dma_start(query_codes[:], q_words[0, 0].rearrange("p q r -> p (q r)").bitcast(I32))
         query_scales = held.tile([P, NQ // 4], I32, name="query_scales", align_bytes=64)
         nc.vector.memset(query_scales[:], 0)
         query_scale_rows = q_scales[0, 0].bitcast(I32).rearrange("(a r) q -> r a q", r=4)
         for r in range(4):
             nc.sync.dma_start(query_scales[r:P:32, :], query_scale_rows[r])
 
-        vs_pool = reused.tile([P, POOL], F32, name="vs_pool", offset=0)
-        nc.sync.dma_start(vs_pool[:, :VS_LOADED], vs[:, :VS_LOADED])
+        nc.sync.dma_start(key_pool[:, LATE_KEYS:], key_words[:, LATE_KEYS:])
 
-        column_list = held.tile([P, PAGES * DV // 16], U16, name="column_list")
-        nc.sync.dma_start(column_list[:], voffs)
+        query_codes = held.tile([P, NQ], I32, name="query_codes", align_bytes=64)
+        nc.sync.dma_start(query_codes[:], q_words[0, 0].rearrange("p q r -> p (q r)").bitcast(I32))
 
-        value_scale_pool = held.tile([P, POOL_PAGES * DV // 4], I32, name="value_scale_pool")
-        nc.vector.memset(value_scale_pool[:], 0)
-        value_scale_rows = v_scales.bitcast(I32).rearrange("u (a r) e -> r a u e", r=4)
+        gate_logits = held.tile([P, DV], F32, name="gate_logits")
+        nc.sync.dma_start(gate_logits[:], og[0])
+
+        identity = held.tile([P, P], F32, name="identity")
+        nc.vector.memset(identity[:], 0.0)
+        make_identity(nc, identity[:], nomemset=True)
+
+        key_scales = held.tile([P, SLOTS // 4], I32, name="key_scales", align_bytes=64)
+        nc.vector.memset(key_scales[:], 0)
+        value_scales = held.tile([P, PAGES * DV // 4], I32, name="value_scales", align_bytes=64)
+        nc.vector.memset(value_scales[:], 0)
+
+        key_scale_rows = held.tile([P, SLOTS], U8, name="key_scale_rows")
+        nc.vector.tensor_copy(key_scale_rows[:], key_scale_pool[:].bitcast(U8).indirect(slot_list[:]))
         for r in range(4):
-            nc.sync.dma_start(
-                value_scale_pool[r:P:32, :].rearrange("a (u e) -> a u e", u=POOL_PAGES), value_scale_rows[r]
-            )
-        value_pool = held.tile([P, POOL_PAGES * DV], I32, name="value_pool")
+            nc.sync.dma_start(key_scales[r:P:32, :], key_scale_rows[:].bitcast(I32)[8 * r : P : 32, :])
+
+        vs_pool = reused.tile([P, POOL], F32, name="vs_pool", align_bytes=64, offset=0)
+        nc.sync.dma_start(vs_pool[:], vs)
+        value_pool = reused.tile([P, POOL_PAGES * DV], I32, name="value_pool", align_bytes=64, offset=POOL * 4)
         nc.sync.dma_start(
             value_pool[:].rearrange("p (u e) -> p u e", u=POOL_PAGES),
             v_words.rearrange("u p e r -> p u (e r)").bitcast(I32),
         )
 
-        identity = held.tile([P, P], F32, name="identity")
-        make_identity(nc, identity[:])
-
-        spread = vs_pool[:, VS_LOADED:].rearrange("r (p j) -> r p j", p=P)
-        for first in range(0, VS_PER_PARTITION, 4):
-            turned = turn_banks.tile([P, 4, P], F32, name="turned")
-            for j in range(4):
-                column = vs_row[:, first + j : first + j + 1].to_broadcast([P, P])
-                nc.tensor.transpose(turned[:, j, :], column, identity[:])
-            nc.scalar.activation(spread[:, :, first : first + 4], turned[:].rearrange("r j p -> r p j"), ACT.Copy)
+        value_scale_rows = held.tile([P, PAGES * DV], U8, name="value_scale_rows")
+        nc.vector.tensor_copy(value_scale_rows[:], value_scale_pool[:].bitcast(U8).indirect(column_list[:]))
+        for r in range(4):
+            nc.sync.dma_start(value_scales[r:P:32, :], value_scale_rows[:].bitcast(I32)[8 * r : P : 32, :])
 
         gate_tanh = held.tile([P, DV], F32, name="gate_tanh")
         nc.scalar.activation(gate_tanh[:], gate_logits[:], ACT.Tanh, scale=0.5)
         gate = held.tile([P, DV], F32, name="gate")
         nc.scalar.activation(gate[:], gate_tanh[:], ACT.Copy, scale=0.5, bias=0.5)
-
-        key_scales = held.tile([P, SLOTS], U8, name="key_scales", align_bytes=64)
-        nc.vector.tensor_copy(key_scales[:], key_scale_pool[:].bitcast(U8).indirect(slot_list[:]))
 
         def page_slots(g):
             return slice(g * PAGE, (g + 1) * PAGE)
@@ -127,7 +126,7 @@ def tile_attend_pkv8q_soft_cap_gate_kernel(
                 lhsT=query_codes[:].bitcast(FP8X4),
                 lhsT_scale=query_scales[:].bitcast(U8),
                 rhs=key_codes[:, page_slots(g)].bitcast(FP8X4),
-                rhs_scale=key_scales[:, page_slots(g)],
+                rhs_scale=key_scales[:].bitcast(U8)[:, page_slots(g)],
                 start=True,
                 stop=True,
             )
@@ -206,17 +205,15 @@ def tile_attend_pkv8q_soft_cap_gate_kernel(
         for g in range(PAGES):
             turn(g)
 
-        value_scales = reused.tile([P, PAGES * DV], U8, name="value_scales", align_bytes=64, offset=PAGES * DV * 4)
-        nc.vector.tensor_copy(value_scales[:], value_scale_pool[:].bitcast(U8).indirect(column_list[:]))
         value_codes = reused.tile([P, PAGES * DV], U32, name="value_codes", align_bytes=64, offset=0)
         nc.vector.tensor_copy(value_codes[:], value_pool[:].bitcast(U32).indirect(column_list[:]))
         for g in range(PAGES):
             quantise(g)
 
-        scaled_sums = stage.tile([P, PAGES], F32, name="scaled_sums", align_bytes=64, offset=0)
+        scaled_sums = ring.tile([P, PAGES], F32, name="weights")
         row_sum = held.tile([P, 1], F32, name="row_sum")
         nc.scalar.activation(scaled_sums[:], page_sums[:], ACT.Copy, scale=exp_neg_max[:], accum_out=row_sum[:])
-        inverse_sum = reused.tile([P, 1], F32, name="inverse_sum", offset=PAGES * DV * 5)
+        inverse_sum = reused.tile([P, 1], F32, name="inverse_sum", align_bytes=64, offset=PAGES * DV * 5)
         nc.vector.reciprocal(inverse_sum[:], row_sum[:])
 
         sums = out_bank.tile([P, DV], F32, name="sums")
@@ -227,7 +224,7 @@ def tile_attend_pkv8q_soft_cap_gate_kernel(
                 lhsT=codes[g][0][:].bitcast(FP8X4),
                 lhsT_scale=codes[g][1][:],
                 rhs=value_codes[:, columns].bitcast(FP8X4),
-                rhs_scale=value_scales[:, columns],
+                rhs_scale=value_scales[:].bitcast(U8)[:, columns],
                 start=(g == 0),
                 stop=(g == PAGES - 1),
             )

@@ -22,7 +22,8 @@ POOL_PAGES = POOL // PAGE
 CAP = 2.0
 LIST_COLS = PAGE // 16
 EARLY_KEYS = POOL // 8
-LATE_KEYS = 3 * POOL // 8
+LATE_KEYS = POOL // 2
+SPREAD = POOL // 4
 
 FLOPS = 2 * NQ * SLOTS * D + 2 * NQ * SLOTS * DV
 
@@ -47,12 +48,17 @@ def tile_attend_pkv8q_soft_cap_gate_kernel(
         key_words = k_words[0].rearrange("p t r -> p (t r)").bitcast(I32)
         nc.sync.dma_start(key_pool[:, :EARLY_KEYS], key_words[:, :EARLY_KEYS])
 
+        column_list = held.tile([P, PAGES * DV // 16], U16, name="column_list")
+        nc.sync.dma_start(column_list[:], voffs)
+        gate_logits = held.tile([P, DV], F32, name="gate_logits")
+        nc.sync.dma_start(gate_logits[:], og[0])
+        vs_runs = held.tile([P, SPREAD // P], F32, name="vs_runs")
+        nc.sync.dma_start(vs_runs[:], vs[0, POOL - SPREAD :].rearrange("(p j) -> p j", p=P))
+
         key_scale_pool = reused.tile([P, POOL // 4], I32, name="key_scale_pool", align_bytes=64, offset=POOL * 4 - 64)
         nc.vector.memset(key_scale_pool[:], 0)
         nc.sync.dma_start(key_scale_pool[0:P:8, :], k_scales[0].bitcast(I32))
 
-        column_list = held.tile([P, PAGES * DV // 16], U16, name="column_list")
-        nc.sync.dma_start(column_list[:], voffs)
         value_scale_pool = held.tile([P, POOL_PAGES * DV // 4], I32, name="value_scale_pool")
         nc.vector.memset(value_scale_pool[:], 0)
         nc.sync.dma_start(
@@ -73,9 +79,6 @@ def tile_attend_pkv8q_soft_cap_gate_kernel(
         query_codes = held.tile([P, NQ], I32, name="query_codes", align_bytes=64)
         nc.sync.dma_start(query_codes[:], q_words[0, 0].rearrange("p q r -> p (q r)").bitcast(I32))
 
-        gate_logits = held.tile([P, DV], F32, name="gate_logits")
-        nc.sync.dma_start(gate_logits[:], og[0])
-
         identity = held.tile([P, P], F32, name="identity")
         nc.vector.memset(identity[:], 0.0)
         make_identity(nc, identity[:], nomemset=True)
@@ -91,7 +94,7 @@ def tile_attend_pkv8q_soft_cap_gate_kernel(
             nc.sync.dma_start(key_scales[r:P:32, :], key_scale_rows[:].bitcast(I32)[8 * r : P : 32, :])
 
         vs_pool = reused.tile([P, POOL], F32, name="vs_pool", align_bytes=64, offset=0)
-        nc.sync.dma_start(vs_pool[:], vs)
+        nc.sync.dma_start(vs_pool[:, : POOL - SPREAD], vs[:, : POOL - SPREAD])
         value_pool = reused.tile([P, POOL_PAGES * DV], I32, name="value_pool", align_bytes=64, offset=POOL * 4)
         nc.sync.dma_start(
             value_pool[:].rearrange("p (u e) -> p u e", u=POOL_PAGES),
@@ -107,6 +110,14 @@ def tile_attend_pkv8q_soft_cap_gate_kernel(
         nc.scalar.activation(gate_tanh[:], gate_logits[:], ACT.Tanh, scale=0.5)
         gate = held.tile([P, DV], F32, name="gate")
         nc.scalar.activation(gate[:], gate_tanh[:], ACT.Copy, scale=0.5, bias=0.5)
+
+        vs_places = vs_pool[:, POOL - SPREAD :].rearrange("m (p h a) -> m h p a", p=P, a=4)
+        for h in range(SPREAD // P // 4):
+            spread = turn_banks.tile([P, 4, P], F32, name="turned")
+            for a in range(4):
+                j = 4 * h + a
+                nc.tensor.transpose(spread[:, a, :], vs_runs[:, j : j + 1].to_broadcast([P, P]), identity[:])
+            nc.scalar.copy(vs_places[:, h], spread[:].rearrange("m a p -> m p a"))
 
         def page_slots(g):
             return slice(g * PAGE, (g + 1) * PAGE)
@@ -139,11 +150,10 @@ def tile_attend_pkv8q_soft_cap_gate_kernel(
         exp_neg_max = held.tile([P, 1], F32, name="exp_neg_max")
         nc.scalar.activation(exp_neg_max[:], row_max[:], ACT.Exp, scale=-CAP)
 
-        first_exp = held.tile([P, PAGE], F32, name="first_exp")
         later_exp = held.tile([P, SLOTS], F32, name="later_exp", tag="keys_then_exp", align_bytes=64)
 
         def exp_capped(first, width):
-            return first_exp[:, first : first + width] if first < PAGE else later_exp[:, first : first + width]
+            return later_exp[:, first : first + width]
 
         page_sums = held.tile([P, PAGES], F32, name="page_sums")
         for g in range(PAGES):

@@ -22,8 +22,9 @@ POOL_PAGES = POOL // PAGE
 CAP = 2.0
 LIST_COLS = PAGE // 16
 EARLY_KEYS = POOL // 8
-LATE_KEYS = POOL // 2
-SPREAD = POOL // 4
+LATE_KEYS = 5 * POOL // 8
+SPREAD = 3 * POOL // 8
+HALF = SLOTS // 2
 
 FLOPS = 2 * NQ * SLOTS * D + 2 * NQ * SLOTS * DV
 
@@ -48,17 +49,16 @@ def tile_attend_pkv8q_soft_cap_gate_kernel(
         key_words = k_words[0].rearrange("p t r -> p (t r)").bitcast(I32)
         nc.sync.dma_start(key_pool[:, :EARLY_KEYS], key_words[:, :EARLY_KEYS])
 
-        column_list = held.tile([P, PAGES * DV // 16], U16, name="column_list")
-        nc.sync.dma_start(column_list[:], voffs)
-        gate_logits = held.tile([P, DV], F32, name="gate_logits")
-        nc.sync.dma_start(gate_logits[:], og[0])
-        vs_runs = held.tile([P, SPREAD // P], F32, name="vs_runs")
-        nc.sync.dma_start(vs_runs[:], vs[0, POOL - SPREAD :].rearrange("(p j) -> p j", p=P))
-
         key_scale_pool = reused.tile([P, POOL // 4], I32, name="key_scale_pool", align_bytes=64, offset=POOL * 4 - 64)
         nc.vector.memset(key_scale_pool[:], 0)
         nc.sync.dma_start(key_scale_pool[0:P:8, :], k_scales[0].bitcast(I32))
 
+        vs_runs = held.tile([P, SPREAD // P], F32, name="vs_runs")
+        nc.sync.dma_start(vs_runs[:], vs[0, POOL - SPREAD :].rearrange("(p j) -> p j", p=P))
+        gate_logits = held.tile([P, DV], F32, name="gate_logits")
+        nc.sync.dma_start(gate_logits[:], og[0])
+        column_list = held.tile([P, PAGES * DV // 16], U16, name="column_list")
+        nc.sync.dma_start(column_list[:], voffs)
         value_scale_pool = held.tile([P, POOL_PAGES * DV // 4], I32, name="value_scale_pool")
         nc.vector.memset(value_scale_pool[:], 0)
         nc.sync.dma_start(
@@ -83,15 +83,19 @@ def tile_attend_pkv8q_soft_cap_gate_kernel(
         nc.vector.memset(identity[:], 0.0)
         make_identity(nc, identity[:], nomemset=True)
 
-        key_scales = held.tile([P, SLOTS // 4], I32, name="key_scales", align_bytes=64)
-        nc.vector.memset(key_scales[:], 0)
+        key_scales = [held.tile([P, HALF // 4], I32, name="key_scales%d" % h, align_bytes=64) for h in range(2)]
+        for plane in key_scales:
+            nc.vector.memset(plane[:], 0)
         value_scales = held.tile([P, PAGES * DV // 4], I32, name="value_scales", align_bytes=64)
         nc.vector.memset(value_scales[:], 0)
 
-        key_scale_rows = held.tile([P, SLOTS], U8, name="key_scale_rows")
-        nc.vector.tensor_copy(key_scale_rows[:], key_scale_pool[:].bitcast(U8).indirect(slot_list[:]))
-        for r in range(4):
-            nc.sync.dma_start(key_scales[r:P:32, :], key_scale_rows[:].bitcast(I32)[8 * r : P : 32, :])
+        for h in range(2):
+            rows = held.tile([P, HALF], U8, name="key_scale_rows%d" % h)
+            nc.vector.tensor_copy(
+                rows[:], key_scale_pool[:].bitcast(U8).indirect(slot_list[:, h * HALF // 16 : (h + 1) * HALF // 16])
+            )
+            for r in range(4):
+                nc.sync.dma_start(key_scales[h][r:P:32, :], rows[:].bitcast(I32)[8 * r : P : 32, :])
 
         vs_pool = reused.tile([P, POOL], F32, name="vs_pool", align_bytes=64, offset=0)
         nc.sync.dma_start(vs_pool[:, : POOL - SPREAD], vs[:, : POOL - SPREAD])
@@ -137,7 +141,7 @@ def tile_attend_pkv8q_soft_cap_gate_kernel(
                 lhsT=query_codes[:].bitcast(FP8X4),
                 lhsT_scale=query_scales[:].bitcast(U8),
                 rhs=key_codes[:, page_slots(g)].bitcast(FP8X4),
-                rhs_scale=key_scales[:].bitcast(U8)[:, page_slots(g)],
+                rhs_scale=key_scales[g // 2][:].bitcast(U8)[:, page_slots(g % 2)],
                 start=True,
                 stop=True,
             )

@@ -25,6 +25,7 @@ EARLY_KEYS = POOL // 8
 LATE_KEYS = 5 * POOL // 8
 SPREAD = 3 * POOL // 8
 HALF = SLOTS // 2
+VS_AT = POOL + 64
 
 FLOPS = 2 * NQ * SLOTS * D + 2 * NQ * SLOTS * DV
 
@@ -49,24 +50,21 @@ def tile_attend_pkv8q_soft_cap_gate_kernel(
         key_words = k_words[0].rearrange("p t r -> p (t r)").bitcast(I32)
         nc.sync.dma_start(key_pool[:, :EARLY_KEYS], key_words[:, :EARLY_KEYS])
 
-        key_scale_pool = reused.tile([P, POOL // 4], I32, name="key_scale_pool", align_bytes=64, offset=POOL * 4 - 64)
+        key_scale_pool = reused.tile([P, POOL // 4], I32, name="key_scale_pool", align_bytes=64, offset=64)
         nc.vector.memset(key_scale_pool[:], 0)
-        nc.sync.dma_start(key_scale_pool[0:P:8, :], k_scales[0].bitcast(I32))
 
         vs_runs = held.tile([P, SPREAD // P], F32, name="vs_runs")
         nc.sync.dma_start(vs_runs[:], vs[0, POOL - SPREAD :].rearrange("(p j) -> p j", p=P))
-        gate_logits = held.tile([P, DV], F32, name="gate_logits")
-        nc.sync.dma_start(gate_logits[:], og[0])
         column_list = held.tile([P, PAGES * DV // 16], U16, name="column_list")
         nc.sync.dma_start(column_list[:], voffs)
+        nc.sync.dma_start(key_scale_pool[0:P:8, :], k_scales[0].bitcast(I32))
+        nc.sync.dma_start(key_pool[:, EARLY_KEYS:LATE_KEYS], key_words[:, EARLY_KEYS:LATE_KEYS])
         value_scale_pool = held.tile([P, POOL_PAGES * DV // 4], I32, name="value_scale_pool")
         nc.vector.memset(value_scale_pool[:], 0)
         nc.sync.dma_start(
             value_scale_pool[0:P:8, :].rearrange("f (u e) -> f u e", u=POOL_PAGES),
             v_scales.bitcast(I32).rearrange("u f e -> f u e"),
         )
-
-        nc.sync.dma_start(key_pool[:, EARLY_KEYS:LATE_KEYS], key_words[:, EARLY_KEYS:LATE_KEYS])
 
         query_scales = held.tile([P, NQ // 4], I32, name="query_scales", align_bytes=64)
         nc.vector.memset(query_scales[:], 0)
@@ -90,30 +88,29 @@ def tile_attend_pkv8q_soft_cap_gate_kernel(
         nc.vector.memset(value_scales[:], 0)
 
         for h in range(2):
-            rows = held.tile([P, HALF], U8, name="key_scale_rows%d" % h)
+            rows = reused.tile([P, HALF], U8, name="key_scale_rows%d" % h, align_bytes=64, offset=VS_AT + POOL * 4 + h * HALF)
             nc.vector.tensor_copy(
                 rows[:], key_scale_pool[:].bitcast(U8).indirect(slot_list[:, h * HALF // 16 : (h + 1) * HALF // 16])
             )
             for r in range(4):
                 nc.sync.dma_start(key_scales[h][r:P:32, :], rows[:].bitcast(I32)[8 * r : P : 32, :])
 
-        vs_pool = reused.tile([P, POOL], F32, name="vs_pool", align_bytes=64, offset=0)
+        vs_pool = reused.tile([P, POOL], F32, name="vs_pool", align_bytes=64, offset=VS_AT)
         nc.sync.dma_start(vs_pool[:, : POOL - SPREAD], vs[:, : POOL - SPREAD])
-        value_pool = reused.tile([P, POOL_PAGES * DV], I32, name="value_pool", align_bytes=64, offset=POOL * 4)
+        value_pool = reused.tile([P, POOL_PAGES * DV], I32, name="value_pool", align_bytes=64, offset=0)
         nc.sync.dma_start(
             value_pool[:].rearrange("p (u e) -> p u e", u=POOL_PAGES),
             v_words.rearrange("u p e r -> p u (e r)").bitcast(I32),
         )
+
+        gate_logits = reused.tile([P, DV], F32, name="gate_logits", align_bytes=64, offset=VS_AT + POOL * 4 + HALF)
+        nc.sync.dma_start(gate_logits[:], og[0])
 
         value_scale_rows = held.tile([P, PAGES * DV], U8, name="value_scale_rows")
         nc.vector.tensor_copy(value_scale_rows[:], value_scale_pool[:].bitcast(U8).indirect(column_list[:]))
         for r in range(4):
             nc.sync.dma_start(value_scales[r:P:32, :], value_scale_rows[:].bitcast(I32)[8 * r : P : 32, :])
 
-        gate_tanh = held.tile([P, DV], F32, name="gate_tanh")
-        nc.scalar.activation(gate_tanh[:], gate_logits[:], ACT.Tanh, scale=0.5)
-        gate = held.tile([P, DV], F32, name="gate")
-        nc.scalar.activation(gate[:], gate_tanh[:], ACT.Copy, scale=0.5, bias=0.5)
 
         vs_places = vs_pool[:, POOL - SPREAD :].rearrange("m (p h a) -> m h p a", p=P, a=4)
         for h in range(SPREAD // P // 4):
@@ -121,7 +118,7 @@ def tile_attend_pkv8q_soft_cap_gate_kernel(
             for a in range(4):
                 j = 4 * h + a
                 nc.tensor.transpose(spread[:, a, :], vs_runs[:, j : j + 1].to_broadcast([P, P]), identity[:])
-            nc.scalar.copy(vs_places[:, h], spread[:].rearrange("m a p -> m p a"))
+            nc.scalar.activation(vs_places[:, h], spread[:].rearrange("m a p -> m p a"), ACT.Copy)
 
         def page_slots(g):
             return slice(g * PAGE, (g + 1) * PAGE)
@@ -219,7 +216,12 @@ def tile_attend_pkv8q_soft_cap_gate_kernel(
         for g in range(PAGES):
             turn(g)
 
-        value_codes = reused.tile([P, PAGES * DV], U32, name="value_codes", align_bytes=64, offset=0)
+        gate_tanh = stage.tile([P, DV], F32, name="gate_tanh", align_bytes=64, offset=0)
+        nc.scalar.activation(gate_tanh[:], gate_logits[:], ACT.Tanh, scale=0.5)
+        gate = held.tile([P, DV], F32, name="gate")
+        nc.scalar.activation(gate[:], gate_tanh[:], ACT.Copy, scale=0.5, bias=0.5)
+
+        value_codes = reused.tile([P, PAGES * DV], U32, name="value_codes", align_bytes=64, offset=VS_AT)
         nc.vector.tensor_copy(value_codes[:], value_pool[:].bitcast(U32).indirect(column_list[:]))
         for g in range(PAGES):
             quantise(g)
@@ -227,7 +229,7 @@ def tile_attend_pkv8q_soft_cap_gate_kernel(
         scaled_sums = ring.tile([P, PAGES], F32, name="weights")
         row_sum = held.tile([P, 1], F32, name="row_sum")
         nc.scalar.activation(scaled_sums[:], page_sums[:], ACT.Copy, scale=exp_neg_max[:], accum_out=row_sum[:])
-        inverse_sum = reused.tile([P, 1], F32, name="inverse_sum", align_bytes=64, offset=PAGES * DV * 5)
+        inverse_sum = reused.tile([P, 1], F32, name="inverse_sum", align_bytes=64, offset=VS_AT + PAGES * DV * 5)
         nc.vector.reciprocal(inverse_sum[:], row_sum[:])
 
         sums = out_bank.tile([P, DV], F32, name="sums")

@@ -20,10 +20,11 @@ PAGE = 512
 PAGES = SLOTS // PAGE
 POOL_PAGES = POOL // PAGE
 CAP = 2.0
-LIST_COLS = PAGE // 16
 EARLY_KEYS = POOL // 8
 LATE_KEYS = 5 * POOL // 8
-SPREAD = 3 * POOL // 8
+SPREAD = POOL // 2
+RUN = 256
+RUNS = SLOTS // RUN
 HALF = SLOTS // 2
 VS_AT = POOL + 64
 
@@ -39,8 +40,7 @@ def tile_attend_pkv8q_soft_cap_gate_kernel(
         reused = ctx.enter_context(tc.tile_pool(name="reused", bufs=1))
         stage = ctx.enter_context(tc.tile_pool(name="stage", bufs=1))
         ring = ctx.enter_context(tc.tile_pool(name="ring", bufs=PAGES))
-        score_banks = ctx.enter_context(tc.psum_pool(name="score_banks", bufs=PAGES))
-        turn_banks = ctx.enter_context(tc.psum_pool(name="turn_banks", bufs=3))
+        banks = ctx.enter_context(tc.psum_pool(name="banks", bufs=7))
         out_bank = ctx.enter_context(tc.psum_pool(name="out_bank", bufs=1))
 
         slot_list = held.tile([P, SLOTS // 16], U16, name="slot_list")
@@ -55,21 +55,13 @@ def tile_attend_pkv8q_soft_cap_gate_kernel(
 
         vs_runs = held.tile([P, SPREAD // P], F32, name="vs_runs")
         nc.sync.dma_start(vs_runs[:], vs[0, POOL - SPREAD :].rearrange("(p j) -> p j", p=P))
-        column_list = held.tile([P, PAGES * DV // 16], U16, name="column_list")
-        nc.sync.dma_start(column_list[:], voffs)
+        query_scales = held.tile([P, NQ // 4], I32, name="query_scales", align_bytes=64)
+        nc.gpsimd.memset(query_scales[:], 0)
+        query_scale_rows = q_scales[0, 0].bitcast(I32).rearrange("(a r) q -> r a q", r=4)
+        nc.sync.dma_start(query_scales[0:P:32, :], query_scale_rows[0])
         nc.sync.dma_start(key_scale_pool[0:P:8, :], k_scales[0].bitcast(I32))
         nc.sync.dma_start(key_pool[:, EARLY_KEYS:LATE_KEYS], key_words[:, EARLY_KEYS:LATE_KEYS])
-        value_scale_pool = held.tile([P, POOL_PAGES * DV // 4], I32, name="value_scale_pool")
-        nc.vector.memset(value_scale_pool[:], 0)
-        nc.sync.dma_start(
-            value_scale_pool[0:P:8, :].rearrange("f (u e) -> f u e", u=POOL_PAGES),
-            v_scales.bitcast(I32).rearrange("u f e -> f u e"),
-        )
-
-        query_scales = held.tile([P, NQ // 4], I32, name="query_scales", align_bytes=64)
-        nc.vector.memset(query_scales[:], 0)
-        query_scale_rows = q_scales[0, 0].bitcast(I32).rearrange("(a r) q -> r a q", r=4)
-        for r in range(4):
+        for r in range(1, 4):
             nc.sync.dma_start(query_scales[r:P:32, :], query_scale_rows[r])
 
         nc.sync.dma_start(key_pool[:, LATE_KEYS:], key_words[:, LATE_KEYS:])
@@ -84,8 +76,8 @@ def tile_attend_pkv8q_soft_cap_gate_kernel(
         key_scales = [held.tile([P, HALF // 4], I32, name="key_scales%d" % h, align_bytes=64) for h in range(2)]
         for plane in key_scales:
             nc.vector.memset(plane[:], 0)
-        value_scales = held.tile([P, PAGES * DV // 4], I32, name="value_scales", align_bytes=64)
-        nc.vector.memset(value_scales[:], 0)
+        value_scale_pool = held.tile([P, POOL_PAGES * DV // 4], I32, name="value_scale_pool")
+        nc.vector.memset(value_scale_pool[:], 0)
 
         for h in range(2):
             rows = reused.tile([P, HALF], U8, name="key_scale_rows%d" % h, align_bytes=64, offset=VS_AT + POOL * 4 + h * HALF)
@@ -97,6 +89,13 @@ def tile_attend_pkv8q_soft_cap_gate_kernel(
 
         vs_pool = reused.tile([P, POOL], F32, name="vs_pool", align_bytes=64, offset=VS_AT)
         nc.sync.dma_start(vs_pool[:, : POOL - SPREAD], vs[:, : POOL - SPREAD])
+        column_list = held.tile([P, PAGES * DV // 16], U16, name="column_list")
+        nc.sync.dma_start(column_list[:], voffs)
+        value_scale_rows = v_scales.bitcast(I32).rearrange("u (a r) e -> r a u e", r=4)
+        for r in range(4):
+            nc.sync.dma_start(
+                value_scale_pool[r:P:32, :].rearrange("a (u e) -> a u e", u=POOL_PAGES), value_scale_rows[r]
+            )
         value_pool = reused.tile([P, POOL_PAGES * DV], I32, name="value_pool", align_bytes=64, offset=0)
         nc.sync.dma_start(
             value_pool[:].rearrange("p (u e) -> p u e", u=POOL_PAGES),
@@ -106,15 +105,10 @@ def tile_attend_pkv8q_soft_cap_gate_kernel(
         gate_logits = reused.tile([P, DV], F32, name="gate_logits", align_bytes=64, offset=VS_AT + POOL * 4 + HALF)
         nc.sync.dma_start(gate_logits[:], og[0])
 
-        value_scale_rows = held.tile([P, PAGES * DV], U8, name="value_scale_rows")
-        nc.vector.tensor_copy(value_scale_rows[:], value_scale_pool[:].bitcast(U8).indirect(column_list[:]))
-        for r in range(4):
-            nc.sync.dma_start(value_scales[r:P:32, :], value_scale_rows[:].bitcast(I32)[8 * r : P : 32, :])
-
 
         vs_places = vs_pool[:, POOL - SPREAD :].rearrange("m (p h a) -> m h p a", p=P, a=4)
         for h in range(SPREAD // P // 4):
-            spread = turn_banks.tile([P, 4, P], F32, name="turned")
+            spread = banks.tile([P, 4, P], F32, name="bank")
             for a in range(4):
                 j = 4 * h + a
                 nc.tensor.transpose(spread[:, a, :], vs_runs[:, j : j + 1].to_broadcast([P, P]), identity[:])
@@ -123,41 +117,40 @@ def tile_attend_pkv8q_soft_cap_gate_kernel(
         def page_slots(g):
             return slice(g * PAGE, (g + 1) * PAGE)
 
-        def page_list(g):
-            return slot_list[:, g * LIST_COLS : (g + 1) * LIST_COLS]
-
         key_codes = held.tile([P, SLOTS], U32, name="key_codes", tag="keys_then_exp", align_bytes=64)
-        for g in range(PAGES):
-            nc.vector.tensor_copy(key_codes[:, page_slots(g)], key_pool[:].bitcast(U32).indirect(page_list(g)))
+        for j in range(RUNS):
+            nc.vector.tensor_copy(
+                key_codes[:, j * RUN : (j + 1) * RUN],
+                key_pool[:].bitcast(U32).indirect(slot_list[:, j * RUN // 16 : (j + 1) * RUN // 16]),
+            )
 
-        capped = held.tile([P, SLOTS + PAGES - 1], F32, name="capped")
-        for g in range(PAGES):
-            scores = score_banks.tile([P, PAGE], F32, name="scores")
+        capped = held.tile([P, SLOTS], F32, name="capped")
+        for j in range(RUNS):
+            scores = banks.tile([P, RUN], F32, name="bank")
+            in_half = j * RUN % HALF
             nc.tensor.matmul_mx(
                 scores[:],
                 lhsT=query_codes[:].bitcast(FP8X4),
                 lhsT_scale=query_scales[:].bitcast(U8),
-                rhs=key_codes[:, page_slots(g)].bitcast(FP8X4),
-                rhs_scale=key_scales[g // 2][:].bitcast(U8)[:, page_slots(g % 2)],
+                rhs=key_codes[:, j * RUN : (j + 1) * RUN].bitcast(FP8X4),
+                rhs_scale=key_scales[j * RUN // HALF][:].bitcast(U8)[:, in_half : in_half + RUN],
                 start=True,
                 stop=True,
             )
-            nc.scalar.activation(capped[:, page_slots(g)], scores[:], ACT.Tanh, scale=1.0 / CAP)
+            nc.scalar.activation(capped[:, j * RUN : (j + 1) * RUN], scores[:], ACT.Tanh, scale=1.0 / CAP)
 
-        for g in range(PAGES - 1):
-            nc.vector.tensor_reduce(capped[:, SLOTS + g : SLOTS + g + 1], capped[:, page_slots(g)], AXIS.X, ALU.max)
-        row_max = held.tile([P, 1], F32, name="row_max")
-        nc.vector.tensor_reduce(row_max[:], capped[:, (PAGES - 1) * PAGE :], AXIS.X, ALU.max)
+        page_max = held.tile([P, PAGES], F32, name="page_max")
+        for g in range(PAGES):
+            nc.vector.tensor_reduce(page_max[:, g : g + 1], capped[:, page_slots(g)], AXIS.X, ALU.max)
         exp_neg_max = held.tile([P, 1], F32, name="exp_neg_max")
-        nc.scalar.activation(exp_neg_max[:], row_max[:], ACT.Exp, scale=-CAP)
-
         later_exp = held.tile([P, SLOTS], F32, name="later_exp", tag="keys_then_exp", align_bytes=64)
 
         def exp_capped(first, width):
             return later_exp[:, first : first + width]
 
         page_sums = held.tile([P, PAGES], F32, name="page_sums")
-        for g in range(PAGES):
+
+        def exponentials(g):
             nc.scalar.activation(
                 exp_capped(g * PAGE, PAGE),
                 capped[:, page_slots(g)],
@@ -193,7 +186,7 @@ def tile_attend_pkv8q_soft_cap_gate_kernel(
 
         def turn(g):
             words = weights[g][:].rearrange("q u s e -> q (u s e)").bitcast(F32)
-            turned = turn_banks.tile([P, 2, NQ], F32, name="turned")
+            turned = banks.tile([P, 2, NQ], F32, name="bank")
             for u in range(2):
                 nc.tensor.transpose(turned[:, u, :], words[:, u * P : (u + 1) * P], identity[:])
             grouped[g] = stage.tile(
@@ -209,7 +202,15 @@ def tile_attend_pkv8q_soft_cap_gate_kernel(
             nc.vector.quantize_mx(out=weight_codes[:].bitcast(FP8X4), scales=weight_scales[:], in_=grouped[g][:])
             codes[g] = (weight_codes, weight_scales)
 
-        for g in range(PAGES):
+        exponentials(0)
+        times_vs(0, 1)
+        exponentials(1)
+        row_max = capped[:, PAGE : PAGE + 1]
+        nc.vector.tensor_reduce(row_max, page_max[:], AXIS.X, ALU.max)
+        nc.scalar.activation(exp_neg_max[:], row_max, ACT.Exp, scale=-CAP)
+        times_vs(1, 1)
+        for g in range(2, PAGES):
+            exponentials(g)
             times_vs(g, 1)
         for g in range(PAGES):
             round_weights(g, g >= PAGES // 2)
@@ -223,6 +224,8 @@ def tile_attend_pkv8q_soft_cap_gate_kernel(
 
         value_codes = reused.tile([P, PAGES * DV], U32, name="value_codes", align_bytes=64, offset=VS_AT)
         nc.vector.tensor_copy(value_codes[:], value_pool[:].bitcast(U32).indirect(column_list[:]))
+        value_scales = reused.tile([P, PAGES * DV], U8, name="value_scales", align_bytes=64, offset=VS_AT + PAGES * DV * 4)
+        nc.vector.tensor_copy(value_scales[:], value_scale_pool[:].bitcast(U8).indirect(column_list[:]))
         for g in range(PAGES):
             quantise(g)
 
@@ -240,7 +243,7 @@ def tile_attend_pkv8q_soft_cap_gate_kernel(
                 lhsT=codes[g][0][:].bitcast(FP8X4),
                 lhsT_scale=codes[g][1][:],
                 rhs=value_codes[:, columns].bitcast(FP8X4),
-                rhs_scale=value_scales[:].bitcast(U8)[:, columns],
+                rhs_scale=value_scales[:, columns],
                 start=(g == 0),
                 stop=(g == PAGES - 1),
             )

@@ -55,13 +55,21 @@ def tile_attend_pkv8q_soft_cap_gate_kernel(
 
         vs_runs = held.tile([P, SPREAD // P], F32, name="vs_runs")
         nc.sync.dma_start(vs_runs[:], vs[0, POOL - SPREAD :].rearrange("(p j) -> p j", p=P))
-        query_scales = held.tile([P, NQ // 4], I32, name="query_scales", align_bytes=64)
-        nc.gpsimd.memset(query_scales[:], 0)
-        query_scale_rows = q_scales[0, 0].bitcast(I32).rearrange("(a r) q -> r a q", r=4)
-        nc.sync.dma_start(query_scales[0:P:32, :], query_scale_rows[0])
+        column_list = held.tile([P, PAGES * DV // 16], U16, name="column_list")
+        nc.sync.dma_start(column_list[:], voffs)
         nc.sync.dma_start(key_scale_pool[0:P:8, :], k_scales[0].bitcast(I32))
         nc.sync.dma_start(key_pool[:, EARLY_KEYS:LATE_KEYS], key_words[:, EARLY_KEYS:LATE_KEYS])
-        for r in range(1, 4):
+        value_scale_pool = held.tile([P, POOL_PAGES * DV // 4], I32, name="value_scale_pool")
+        nc.vector.memset(value_scale_pool[:], 0)
+        nc.sync.dma_start(
+            value_scale_pool[0:P:8, :].rearrange("f (u e) -> f u e", u=POOL_PAGES),
+            v_scales.bitcast(I32).rearrange("u f e -> f u e"),
+        )
+
+        query_scales = held.tile([P, NQ // 4], I32, name="query_scales", align_bytes=64)
+        nc.vector.memset(query_scales[:], 0)
+        query_scale_rows = q_scales[0, 0].bitcast(I32).rearrange("(a r) q -> r a q", r=4)
+        for r in range(4):
             nc.sync.dma_start(query_scales[r:P:32, :], query_scale_rows[r])
 
         nc.sync.dma_start(key_pool[:, LATE_KEYS:], key_words[:, LATE_KEYS:])
@@ -76,8 +84,8 @@ def tile_attend_pkv8q_soft_cap_gate_kernel(
         key_scales = [held.tile([P, HALF // 4], I32, name="key_scales%d" % h, align_bytes=64) for h in range(2)]
         for plane in key_scales:
             nc.vector.memset(plane[:], 0)
-        value_scale_pool = held.tile([P, POOL_PAGES * DV // 4], I32, name="value_scale_pool")
-        nc.vector.memset(value_scale_pool[:], 0)
+        value_scales = held.tile([P, PAGES * DV // 4], I32, name="value_scales", align_bytes=64)
+        nc.vector.memset(value_scales[:], 0)
 
         for h in range(2):
             rows = reused.tile([P, HALF], U8, name="key_scale_rows%d" % h, align_bytes=64, offset=VS_AT + POOL * 4 + h * HALF)
@@ -89,13 +97,6 @@ def tile_attend_pkv8q_soft_cap_gate_kernel(
 
         vs_pool = reused.tile([P, POOL], F32, name="vs_pool", align_bytes=64, offset=VS_AT)
         nc.sync.dma_start(vs_pool[:, : POOL - SPREAD], vs[:, : POOL - SPREAD])
-        column_list = held.tile([P, PAGES * DV // 16], U16, name="column_list")
-        nc.sync.dma_start(column_list[:], voffs)
-        value_scale_rows = v_scales.bitcast(I32).rearrange("u (a r) e -> r a u e", r=4)
-        for r in range(4):
-            nc.sync.dma_start(
-                value_scale_pool[r:P:32, :].rearrange("a (u e) -> a u e", u=POOL_PAGES), value_scale_rows[r]
-            )
         value_pool = reused.tile([P, POOL_PAGES * DV], I32, name="value_pool", align_bytes=64, offset=0)
         nc.sync.dma_start(
             value_pool[:].rearrange("p (u e) -> p u e", u=POOL_PAGES),
@@ -104,6 +105,11 @@ def tile_attend_pkv8q_soft_cap_gate_kernel(
 
         gate_logits = reused.tile([P, DV], F32, name="gate_logits", align_bytes=64, offset=VS_AT + POOL * 4 + HALF)
         nc.sync.dma_start(gate_logits[:], og[0])
+
+        value_scale_rows = held.tile([P, PAGES * DV], U8, name="value_scale_rows")
+        nc.vector.tensor_copy(value_scale_rows[:], value_scale_pool[:].bitcast(U8).indirect(column_list[:]))
+        for r in range(4):
+            nc.sync.dma_start(value_scales[r:P:32, :], value_scale_rows[:].bitcast(I32)[8 * r : P : 32, :])
 
 
         vs_places = vs_pool[:, POOL - SPREAD :].rearrange("m (p h a) -> m h p a", p=P, a=4)
@@ -224,8 +230,6 @@ def tile_attend_pkv8q_soft_cap_gate_kernel(
 
         value_codes = reused.tile([P, PAGES * DV], U32, name="value_codes", align_bytes=64, offset=VS_AT)
         nc.vector.tensor_copy(value_codes[:], value_pool[:].bitcast(U32).indirect(column_list[:]))
-        value_scales = reused.tile([P, PAGES * DV], U8, name="value_scales", align_bytes=64, offset=VS_AT + PAGES * DV * 4)
-        nc.vector.tensor_copy(value_scales[:], value_scale_pool[:].bitcast(U8).indirect(column_list[:]))
         for g in range(PAGES):
             quantise(g)
 
@@ -243,7 +247,7 @@ def tile_attend_pkv8q_soft_cap_gate_kernel(
                 lhsT=codes[g][0][:].bitcast(FP8X4),
                 lhsT_scale=codes[g][1][:],
                 rhs=value_codes[:, columns].bitcast(FP8X4),
-                rhs_scale=value_scales[:, columns],
+                rhs_scale=value_scales[:].bitcast(U8)[:, columns],
                 start=(g == 0),
                 stop=(g == PAGES - 1),
             )

@@ -22,7 +22,7 @@ POOL_PAGES = POOL // PAGE
 CAP = 2.0
 EARLY_KEYS = POOL // 8
 LATE_KEYS = 5 * POOL // 8
-SPREAD = POOL // 2
+SPREAD = 3 * POOL // 4
 RUN = 256
 RUNS = SLOTS // RUN
 HALF = SLOTS // 2
@@ -39,6 +39,7 @@ def tile_attend_pkv8q_soft_cap_gate_kernel(
         held = ctx.enter_context(tc.tile_pool(name="held", bufs=1))
         reused = ctx.enter_context(tc.tile_pool(name="reused", bufs=1))
         stage = ctx.enter_context(tc.tile_pool(name="stage", bufs=1))
+        keys_then_exp = ctx.enter_context(tc.tile_pool(name="keys_then_exp", bufs=1))
         ring = ctx.enter_context(tc.tile_pool(name="ring", bufs=PAGES))
         banks = ctx.enter_context(tc.psum_pool(name="banks", bufs=7))
         out_bank = ctx.enter_context(tc.psum_pool(name="out_bank", bufs=1))
@@ -123,36 +124,48 @@ def tile_attend_pkv8q_soft_cap_gate_kernel(
         def page_slots(g):
             return slice(g * PAGE, (g + 1) * PAGE)
 
-        key_codes = held.tile([P, SLOTS], U32, name="key_codes", tag="keys_then_exp", align_bytes=64)
-        for j in range(RUNS):
+        key_codes = [
+            keys_then_exp.tile([P, PAGE], U32, name="key_codes%d" % g, align_bytes=64, offset=g * PAGE * 4)
+            for g in range(PAGES)
+        ]
+        for g in range(PAGES):
             nc.vector.tensor_copy(
-                key_codes[:, j * RUN : (j + 1) * RUN],
-                key_pool[:].bitcast(U32).indirect(slot_list[:, j * RUN // 16 : (j + 1) * RUN // 16]),
+                key_codes[g][:],
+                key_pool[:].bitcast(U32).indirect(slot_list[:, g * PAGE // 16 : (g + 1) * PAGE // 16]),
             )
 
-        capped = held.tile([P, SLOTS], F32, name="capped")
-        for j in range(RUNS):
+        capped = held.tile([P, SLOTS + PAGES - 1], F32, name="capped")
+
+        def score_and_cap(j):
             scores = banks.tile([P, RUN], F32, name="bank")
             in_half = j * RUN % HALF
+            in_page = j * RUN % PAGE
             nc.tensor.matmul_mx(
                 scores[:],
                 lhsT=query_codes[:].bitcast(FP8X4),
                 lhsT_scale=query_scales[:].bitcast(U8),
-                rhs=key_codes[:, j * RUN : (j + 1) * RUN].bitcast(FP8X4),
+                rhs=key_codes[j * RUN // PAGE][:, in_page : in_page + RUN].bitcast(FP8X4),
                 rhs_scale=key_scales[j * RUN // HALF][:].bitcast(U8)[:, in_half : in_half + RUN],
                 start=True,
                 stop=True,
             )
             nc.scalar.activation(capped[:, j * RUN : (j + 1) * RUN], scores[:], ACT.Tanh, scale=1.0 / CAP)
 
-        page_max = held.tile([P, PAGES], F32, name="page_max")
-        for g in range(PAGES):
-            nc.vector.tensor_reduce(page_max[:, g : g + 1], capped[:, page_slots(g)], AXIS.X, ALU.max)
+        runs_a_page = PAGE // RUN
+        for j in range(RUNS - runs_a_page):
+            score_and_cap(j)
+        for g in range(PAGES - 1):
+            nc.vector.tensor_reduce(capped[:, SLOTS + g : SLOTS + g + 1], capped[:, page_slots(g)], AXIS.X, ALU.max)
         exp_neg_max = held.tile([P, 1], F32, name="exp_neg_max")
-        later_exp = held.tile([P, SLOTS], F32, name="later_exp", tag="keys_then_exp", align_bytes=64)
+        first_exp = keys_then_exp.tile([P, PAGE], F32, name="first_exp", align_bytes=64, offset=(PAGES - 2) * PAGE * 4)
+        later_exp = keys_then_exp.tile(
+            [P, SLOTS - PAGE], F32, name="later_exp", align_bytes=64, offset=(PAGES - 1) * PAGE * 4
+        )
 
         def exp_capped(first, width):
-            return later_exp[:, first : first + width]
+            if first < PAGE:
+                return first_exp[:, first : first + width]
+            return later_exp[:, first - PAGE : first - PAGE + width]
 
         page_sums = held.tile([P, PAGES], F32, name="page_sums")
 
@@ -210,12 +223,12 @@ def tile_attend_pkv8q_soft_cap_gate_kernel(
 
         exponentials(0)
         times_vs(0, 1)
-        exponentials(1)
-        row_max = capped[:, PAGE : PAGE + 1]
-        nc.vector.tensor_reduce(row_max, page_max[:], AXIS.X, ALU.max)
-        nc.scalar.activation(exp_neg_max[:], row_max, ACT.Exp, scale=-CAP)
-        times_vs(1, 1)
-        for g in range(2, PAGES):
+        for j in range(RUNS - runs_a_page, RUNS):
+            score_and_cap(j)
+        row_max = held.tile([P, 1], F32, name="row_max")
+        nc.vector.tensor_reduce(row_max[:], capped[:, (PAGES - 1) * PAGE :], AXIS.X, ALU.max)
+        nc.scalar.activation(exp_neg_max[:], row_max[:], ACT.Exp, scale=-CAP)
+        for g in range(1, PAGES):
             exponentials(g)
             times_vs(g, 1)
         for g in range(PAGES):

@@ -23,8 +23,6 @@ CAP = 2.0
 EARLY_KEYS = POOL // 8
 LATE_KEYS = 5 * POOL // 8
 SPREAD = 3 * POOL // 4
-RUN = 256
-RUNS = SLOTS // RUN
 HALF = SLOTS // 2
 VS_AT = POOL + 64
 
@@ -88,6 +86,7 @@ def tile_attend_pkv8q_soft_cap_gate_kernel(
         value_scales = held.tile([P, PAGES * DV // 4], I32, name="value_scales", align_bytes=64)
         nc.vector.memset(value_scales[:], 0)
 
+        vs_pool = reused.tile([P, POOL], F32, name="vs_pool", align_bytes=64, offset=VS_AT)
         for h in range(2):
             rows = reused.tile([P, HALF], U8, name="key_scale_rows%d" % h, align_bytes=64, offset=VS_AT + POOL * 4 + h * HALF)
             nc.vector.tensor_copy(
@@ -95,9 +94,9 @@ def tile_attend_pkv8q_soft_cap_gate_kernel(
             )
             for r in range(4):
                 nc.sync.dma_start(key_scales[h][r:P:32, :], rows[:].bitcast(I32)[8 * r : P : 32, :])
+            if h == 0:
+                nc.sync.dma_start(vs_pool[:, : POOL - SPREAD], vs[:, : POOL - SPREAD])
 
-        vs_pool = reused.tile([P, POOL], F32, name="vs_pool", align_bytes=64, offset=VS_AT)
-        nc.sync.dma_start(vs_pool[:, : POOL - SPREAD], vs[:, : POOL - SPREAD])
         value_pool = reused.tile([P, POOL_PAGES * DV], I32, name="value_pool", align_bytes=64, offset=0)
         nc.sync.dma_start(
             value_pool[:].rearrange("p (u e) -> p u e", u=POOL_PAGES),
@@ -128,54 +127,53 @@ def tile_attend_pkv8q_soft_cap_gate_kernel(
             keys_then_exp.tile([P, PAGE], U32, name="key_codes%d" % g, align_bytes=64, offset=g * PAGE * 4)
             for g in range(PAGES)
         ]
-        for g in range(PAGES):
+        runs = [(0, PAGE // 2), (PAGE // 2, PAGE // 2)] + [(g * PAGE, PAGE) for g in range(1, PAGES)]
+        for first, width in runs:
             nc.vector.tensor_copy(
-                key_codes[g][:],
-                key_pool[:].bitcast(U32).indirect(slot_list[:, g * PAGE // 16 : (g + 1) * PAGE // 16]),
+                key_codes[first // PAGE][:, first % PAGE : first % PAGE + width],
+                key_pool[:].bitcast(U32).indirect(slot_list[:, first // 16 : (first + width) // 16]),
             )
 
         capped = held.tile([P, SLOTS + PAGES - 1], F32, name="capped")
 
-        def score_and_cap(j):
-            scores = banks.tile([P, RUN], F32, name="bank")
-            in_half = j * RUN % HALF
-            in_page = j * RUN % PAGE
+        def score_and_cap(first, width):
+            scores = banks.tile([P, width], F32, name="bank")
             nc.tensor.matmul_mx(
                 scores[:],
                 lhsT=query_codes[:].bitcast(FP8X4),
                 lhsT_scale=query_scales[:].bitcast(U8),
-                rhs=key_codes[j * RUN // PAGE][:, in_page : in_page + RUN].bitcast(FP8X4),
-                rhs_scale=key_scales[j * RUN // HALF][:].bitcast(U8)[:, in_half : in_half + RUN],
+                rhs=key_codes[first // PAGE][:, first % PAGE : first % PAGE + width].bitcast(FP8X4),
+                rhs_scale=key_scales[first // HALF][:].bitcast(U8)[:, first % HALF : first % HALF + width],
                 start=True,
                 stop=True,
             )
-            nc.scalar.activation(capped[:, j * RUN : (j + 1) * RUN], scores[:], ACT.Tanh, scale=1.0 / CAP)
+            nc.scalar.activation(capped[:, first : first + width], scores[:], ACT.Tanh, scale=1.0 / CAP)
 
-        runs_a_page = PAGE // RUN
-        for j in range(RUNS - runs_a_page):
-            score_and_cap(j)
-        for g in range(PAGES - 1):
+        def page_maximum(g):
             nc.vector.tensor_reduce(capped[:, SLOTS + g : SLOTS + g + 1], capped[:, page_slots(g)], AXIS.X, ALU.max)
+
         exp_neg_max = held.tile([P, 1], F32, name="exp_neg_max")
-        first_exp = keys_then_exp.tile([P, PAGE], F32, name="first_exp", align_bytes=64, offset=(PAGES - 2) * PAGE * 4)
-        later_exp = keys_then_exp.tile(
-            [P, SLOTS - PAGE], F32, name="later_exp", align_bytes=64, offset=(PAGES - 1) * PAGE * 4
-        )
+        first_exp = held.tile([P, PAGE], F32, name="first_exp")
+        second_exp = keys_then_exp.tile([P, PAGE], F32, name="second_exp", align_bytes=64, offset=(PAGES - 2) * PAGE * 4)
+        later_exp = keys_then_exp.tile([P, HALF], F32, name="later_exp", align_bytes=64, offset=(PAGES - 1) * PAGE * 4)
 
         def exp_capped(first, width):
             if first < PAGE:
                 return first_exp[:, first : first + width]
-            return later_exp[:, first - PAGE : first - PAGE + width]
+            if first < HALF:
+                return second_exp[:, first - PAGE : first - PAGE + width]
+            return later_exp[:, first - HALF : first - HALF + width]
 
-        page_sums = held.tile([P, PAGES], F32, name="page_sums")
+        run_sums = held.tile([P, len(runs)], F32, name="run_sums")
 
-        def exponentials(g):
+        def exponentials(j):
+            first, width = runs[j]
             nc.scalar.activation(
-                exp_capped(g * PAGE, PAGE),
-                capped[:, page_slots(g)],
+                exp_capped(first, width),
+                capped[:, first : first + width],
                 ACT.Exp,
                 scale=CAP,
-                accum_out=page_sums[:, g : g + 1],
+                accum_out=run_sums[:, j : j + 1],
             )
 
         scaled = {}
@@ -221,16 +219,26 @@ def tile_attend_pkv8q_soft_cap_gate_kernel(
             nc.vector.quantize_mx(out=weight_codes[:].bitcast(FP8X4), scales=weight_scales[:], in_=grouped[g][:])
             codes[g] = (weight_codes, weight_scales)
 
+        score_and_cap(*runs[0])
+        score_and_cap(*runs[1])
+        page_maximum(0)
         exponentials(0)
+        exponentials(1)
         times_vs(0, 1)
-        for j in range(RUNS - runs_a_page, RUNS):
-            score_and_cap(j)
+        score_and_cap(*runs[2])
+        page_maximum(1)
+        score_and_cap(*runs[3])
+        page_maximum(2)
+        exponentials(2)
+        times_vs(1, 1)
+        score_and_cap(*runs[4])
         row_max = held.tile([P, 1], F32, name="row_max")
         nc.vector.tensor_reduce(row_max[:], capped[:, (PAGES - 1) * PAGE :], AXIS.X, ALU.max)
+        exponentials(3)
+        times_vs(2, 1)
+        exponentials(4)
+        times_vs(3, 1)
         nc.scalar.activation(exp_neg_max[:], row_max[:], ACT.Exp, scale=-CAP)
-        for g in range(1, PAGES):
-            exponentials(g)
-            times_vs(g, 1)
         for g in range(PAGES):
             round_weights(g, g >= PAGES // 2)
         for g in range(PAGES):
@@ -246,9 +254,9 @@ def tile_attend_pkv8q_soft_cap_gate_kernel(
         for g in range(PAGES):
             quantise(g)
 
-        scaled_sums = ring.tile([P, PAGES], F32, name="weights")
+        scaled_sums = ring.tile([P, len(runs)], F32, name="weights")
         row_sum = held.tile([P, 1], F32, name="row_sum")
-        nc.scalar.activation(scaled_sums[:], page_sums[:], ACT.Copy, scale=exp_neg_max[:], accum_out=row_sum[:])
+        nc.scalar.activation(scaled_sums[:], run_sums[:], ACT.Copy, scale=exp_neg_max[:], accum_out=row_sum[:])
         inverse_sum = reused.tile([P, 1], F32, name="inverse_sum", align_bytes=64, offset=VS_AT + PAGES * DV * 5)
         nc.vector.reciprocal(inverse_sum[:], row_sum[:])
 

@@ -207,11 +207,10 @@ def tile_attend_pkv8q_soft_cap_gate_kernel(
             for u in range(2):
                 nc.tensor.transpose(turned[:, u, :], words[:, u * P : (u + 1) * P], identity[:])
             grouped[g] = stage.tile(
-                [P, NQ * 4], BF16, name="grouped%d" % g, align_bytes=64, offset=(1 if g == 0 else PAGES + g) * PAGE * 4
+                [P, NQ * 4], BF16, name="grouped%d" % g, align_bytes=64, offset=(PAGES + g) * PAGE * 4
             )
-            nc.scalar.copy(
-                grouped[g][:].bitcast(F32).rearrange("s (q u) -> s q u", u=2), turned[:].rearrange("s u q -> s q u")
-            )
+            copy = nc.vector.tensor_copy if g == PAGES - 2 else nc.scalar.copy
+            copy(grouped[g][:].bitcast(F32).rearrange("s (q u) -> s q u", u=2), turned[:].rearrange("s u q -> s q u"))
 
         def quantise(g):
             weight_codes = ring.tile([P, NQ], U32, name="weight_codes", align_bytes=64)
@@ -240,7 +239,7 @@ def tile_attend_pkv8q_soft_cap_gate_kernel(
         times_vs(3, 1)
         nc.scalar.activation(exp_neg_max[:], row_max[:], ACT.Exp, scale=-CAP)
         for g in range(PAGES):
-            round_weights(g, g >= PAGES // 2)
+            round_weights(g, g > 0)
         for g in range(PAGES):
             turn(g)
 
@@ -254,7 +253,7 @@ def tile_attend_pkv8q_soft_cap_gate_kernel(
         for g in range(PAGES):
             quantise(g)
 
-        scaled_sums = ring.tile([P, len(runs)], F32, name="weights")
+        scaled_sums = held.tile([P, len(runs)], F32, name="scaled_sums")
         row_sum = held.tile([P, 1], F32, name="row_sum")
         nc.scalar.activation(scaled_sums[:], run_sums[:], ACT.Copy, scale=exp_neg_max[:], accum_out=row_sum[:])
         inverse_sum = reused.tile([P, 1], F32, name="inverse_sum", align_bytes=64, offset=VS_AT + PAGES * DV * 5)

@@ -24,6 +24,7 @@ EARLY_KEYS = POOL // 8
 LATE_KEYS = 5 * POOL // 8
 SPREAD = 3 * POOL // 4
 HALF = SLOTS // 2
+ROWS_AT = 32
 VS_AT = POOL + 64
 
 FLOPS = 2 * NQ * SLOTS * D + 2 * NQ * SLOTS * DV
@@ -56,12 +57,12 @@ def tile_attend_pkv8q_soft_cap_gate_kernel(
         nc.sync.dma_start(vs_runs[:], vs[0, POOL - SPREAD :].rearrange("(p j) -> p j", p=P))
         column_list = held.tile([P, PAGES * DV // 16], U16, name="column_list")
         nc.sync.dma_start(column_list[:], voffs)
-        nc.sync.dma_start(key_scale_pool[0:P:8, :], k_scales[0].bitcast(I32))
+        nc.sync.dma_start(key_scale_pool[ROWS_AT : ROWS_AT + 64 : 4, :], k_scales[0].bitcast(I32))
         nc.sync.dma_start(key_pool[:, EARLY_KEYS:LATE_KEYS], key_words[:, EARLY_KEYS:LATE_KEYS])
         value_scale_pool = held.tile([P, POOL_PAGES * DV // 4], I32, name="value_scale_pool")
         nc.vector.memset(value_scale_pool[:], 0)
         nc.sync.dma_start(
-            value_scale_pool[0:P:8, :].rearrange("f (u e) -> f u e", u=POOL_PAGES),
+            value_scale_pool[ROWS_AT : ROWS_AT + 64 : 4, :].rearrange("f (u e) -> f u e", u=POOL_PAGES),
             v_scales.bitcast(I32).rearrange("u f e -> f u e"),
         )
 
@@ -93,7 +94,7 @@ def tile_attend_pkv8q_soft_cap_gate_kernel(
                 rows[:], key_scale_pool[:].bitcast(U8).indirect(slot_list[:, h * HALF // 16 : (h + 1) * HALF // 16])
             )
             for r in range(4):
-                nc.sync.dma_start(key_scales[h][r:P:32, :], rows[:].bitcast(I32)[8 * r : P : 32, :])
+                nc.sync.dma_start(key_scales[h][r:P:32, :], rows[:].bitcast(I32)[ROWS_AT + 4 * r : ROWS_AT + 64 : 16, :])
             if h == 0:
                 nc.sync.dma_start(vs_pool[:, : POOL - SPREAD], vs[:, : POOL - SPREAD])
 
@@ -109,7 +110,7 @@ def tile_attend_pkv8q_soft_cap_gate_kernel(
         value_scale_rows = held.tile([P, PAGES * DV], U8, name="value_scale_rows")
         nc.vector.tensor_copy(value_scale_rows[:], value_scale_pool[:].bitcast(U8).indirect(column_list[:]))
         for r in range(4):
-            nc.sync.dma_start(value_scales[r:P:32, :], value_scale_rows[:].bitcast(I32)[8 * r : P : 32, :])
+            nc.sync.dma_start(value_scales[r:P:32, :], value_scale_rows[:].bitcast(I32)[ROWS_AT + 4 * r : ROWS_AT + 64 : 16, :])
 
 
         vs_places = vs_pool[:, POOL - SPREAD :].rearrange("m (p h a) -> m h p a", p=P, a=4)

@@ -210,8 +210,9 @@ def tile_attend_pkv8q_soft_cap_gate_kernel(
             grouped[g] = stage.tile(
                 [P, NQ * 4], BF16, name="grouped%d" % g, align_bytes=64, offset=(PAGES + g) * PAGE * 4
             )
-            copy = nc.vector.tensor_copy if g == PAGES - 2 else nc.scalar.copy
-            copy(grouped[g][:].bitcast(F32).rearrange("s (q u) -> s q u", u=2), turned[:].rearrange("s u q -> s q u"))
+            nc.scalar.copy(
+                grouped[g][:].bitcast(F32).rearrange("s (q u) -> s q u", u=2), turned[:].rearrange("s u q -> s q u")
+            )
 
         def quantise(g):
             weight_codes = ring.tile([P, NQ], U32, name="weight_codes", align_bytes=64)
@@ -232,22 +233,23 @@ def tile_attend_pkv8q_soft_cap_gate_kernel(
         exponentials(2)
         times_vs(1, 1)
         score_and_cap(*runs[4])
-        row_max = held.tile([P, 1], F32, name="row_max")
+        row_max = stage.tile([P, 1], F32, name="row_max", align_bytes=64, offset=(PAGES - 1) * PAGE * 4)
         nc.vector.tensor_reduce(row_max[:], capped[:, (PAGES - 1) * PAGE :], AXIS.X, ALU.max)
         exponentials(3)
         times_vs(2, 1)
         exponentials(4)
-        times_vs(3, 1)
         nc.scalar.activation(exp_neg_max[:], row_max[:], ACT.Exp, scale=-CAP)
-        for g in range(PAGES):
-            round_weights(g, g > 0)
+        gate_tanh = capped[:, HALF : HALF + DV]
+        nc.scalar.activation(gate_tanh, gate_logits[:], ACT.Tanh, scale=0.5)
+        round_weights(0, True)
+        times_vs(3, 1)
+        for g in range(1, PAGES):
+            round_weights(g, g > 1)
         for g in range(PAGES):
             turn(g)
 
-        gate_tanh = stage.tile([P, DV], F32, name="gate_tanh", align_bytes=64, offset=0)
-        nc.scalar.activation(gate_tanh[:], gate_logits[:], ACT.Tanh, scale=0.5)
         gate = held.tile([P, DV], F32, name="gate")
-        nc.scalar.activation(gate[:], gate_tanh[:], ACT.Copy, scale=0.5, bias=0.5)
+        nc.scalar.activation(gate[:], gate_tanh, ACT.Copy, scale=0.5, bias=0.5)
 
         value_codes = reused.tile([P, PAGES * DV], U32, name="value_codes", align_bytes=64, offset=VS_AT)
         nc.vector.tensor_copy(value_codes[:], value_pool[:].bitcast(U32).indirect(column_list[:]))

@@ -194,13 +194,14 @@ def tile_attend_pkv8q_soft_cap_gate_kernel(
                     ALU.mult,
                 )
 
-        def round_weights(g, on_vector):
-            weights[g] = ring.tile([P, 2, P, 2], BF16, name="weights")
-            source = scaled[g][:].rearrange("q (s u e) -> q u s e", u=2, e=2)
+        def round_weights(g, halves, on_vector):
+            if g not in weights:
+                weights[g] = ring.tile([P, 2, P, 2], BF16, name="weights")
+            source = scaled[g][:].rearrange("q (s u e) -> q u s e", u=2, e=2)[:, halves]
             if on_vector:
-                nc.vector.tensor_scalar(weights[g][:], source, exp_neg_max[:], None, ALU.mult)
+                nc.vector.tensor_scalar(weights[g][:, halves], source, exp_neg_max[:], None, ALU.mult)
             else:
-                nc.scalar.activation(weights[g][:], source, ACT.Copy, scale=exp_neg_max[:])
+                nc.scalar.activation(weights[g][:, halves], source, ACT.Copy, scale=exp_neg_max[:])
 
         def turn(g):
             words = weights[g][:].rearrange("q u s e -> q (u s e)").bitcast(F32)
@@ -241,10 +242,14 @@ def tile_attend_pkv8q_soft_cap_gate_kernel(
         nc.scalar.activation(exp_neg_max[:], row_max[:], ACT.Exp, scale=-CAP)
         gate_tanh = capped[:, HALF : HALF + DV]
         nc.scalar.activation(gate_tanh, gate_logits[:], ACT.Tanh, scale=0.5)
-        round_weights(0, True)
+        low, high, both = slice(0, 1), slice(1, 2), slice(0, 2)
+        round_weights(0, low, True)
+        round_weights(0, high, False)
         times_vs(3, 1)
-        for g in range(1, PAGES):
-            round_weights(g, g > 1)
+        for half in (low, high):
+            round_weights(1, half, False)
+        for g in range(2, PAGES):
+            round_weights(g, both, True)
         for g in range(PAGES):
             turn(g)
 

from contextlib import ExitStack

import concourse.mybir as mybir
from concourse.masks import make_identity

F32 = mybir.dt.float32
BF16 = mybir.dt.bfloat16
I32 = mybir.dt.int32
U32 = mybir.dt.uint32
U16 = mybir.dt.uint16
U8 = mybir.dt.uint8
FP8X4 = mybir.dt.float8_e4m3fn_x4
ACT = mybir.ActivationFunctionType
ALU = mybir.AluOpType
AXIS = mybir.AxisListType

P = 128
NQ, SLOTS, POOL, D, DV = 128, 2048, 4096, 512, 128
PAGE = 512
PAGES = SLOTS // PAGE
POOL_PAGES = POOL // PAGE
CAP = 2.0
EARLY_KEYS = POOL // 8
LATE_KEYS = 5 * POOL // 8
SPREAD = 3 * POOL // 4
HALF = SLOTS // 2
ROWS_AT = 32
VS_AT = POOL + 64

FLOPS = 2 * NQ * SLOTS * D + 2 * NQ * SLOTS * DV


def tile_attend_pkv8q_soft_cap_gate_kernel(
    tc, q_words, q_scales, k_words, k_scales, v_words, v_scales, vs, og, offs, voffs, out
):
    nc = tc.nc
    with ExitStack() as ctx:
        held = ctx.enter_context(tc.tile_pool(name="held", bufs=1))
        reused = ctx.enter_context(tc.tile_pool(name="reused", bufs=1))
        stage = ctx.enter_context(tc.tile_pool(name="stage", bufs=1))
        keys_then_exp = ctx.enter_context(tc.tile_pool(name="keys_then_exp", bufs=1))
        ring = ctx.enter_context(tc.tile_pool(name="ring", bufs=PAGES))
        banks = ctx.enter_context(tc.psum_pool(name="banks", bufs=7))
        out_bank = ctx.enter_context(tc.psum_pool(name="out_bank", bufs=1))

        slot_list = held.tile([P, SLOTS // 16], U16, name="slot_list")
        nc.sync.dma_start(slot_list[:], offs)

        key_pool = held.tile([P, POOL], I32, name="key_pool")
        key_words = k_words[0].rearrange("p t r -> p (t r)").bitcast(I32)
        nc.sync.dma_start(key_pool[:, :EARLY_KEYS], key_words[:, :EARLY_KEYS])

        key_scale_pool = reused.tile([P, POOL // 4], I32, name="key_scale_pool", align_bytes=64, offset=64)
        nc.vector.memset(key_scale_pool[:], 0)

        vs_runs = held.tile([P, SPREAD // P], F32, name="vs_runs")
        nc.sync.dma_start(vs_runs[:], vs[0, POOL - SPREAD :].rearrange("(p j) -> p j", p=P))
        column_list = held.tile([P, PAGES * DV // 16], U16, name="column_list")
        nc.sync.dma_start(column_list[:], voffs)
        nc.sync.dma_start(key_scale_pool[ROWS_AT : ROWS_AT + 64 : 4, :], k_scales[0].bitcast(I32))
        nc.sync.dma_start(key_pool[:, EARLY_KEYS:LATE_KEYS], key_words[:, EARLY_KEYS:LATE_KEYS])
        value_scale_pool = held.tile([P, POOL_PAGES * DV // 4], I32, name="value_scale_pool")
        nc.vector.memset(value_scale_pool[:], 0)
        nc.sync.dma_start(
            value_scale_pool[ROWS_AT : ROWS_AT + 64 : 4, :].rearrange("f (u e) -> f u e", u=POOL_PAGES),
            v_scales.bitcast(I32).rearrange("u f e -> f u e"),
        )

        query_scales = held.tile([P, NQ // 4], I32, name="query_scales", align_bytes=64)
        nc.vector.memset(query_scales[:], 0)
        query_scale_rows = q_scales[0, 0].bitcast(I32).rearrange("(a r) q -> r a q", r=4)
        for r in range(4):
            nc.sync.dma_start(query_scales[r:P:32, :], query_scale_rows[r])

        nc.sync.dma_start(key_pool[:, LATE_KEYS:], key_words[:, LATE_KEYS:])

        query_codes = held.tile([P, NQ], I32, name="query_codes", align_bytes=64)
        nc.sync.dma_start(query_codes[:], q_words[0, 0].rearrange("p q r -> p (q r)").bitcast(I32))

        identity = held.tile([P, P], F32, name="identity")
        nc.vector.memset(identity[:], 0.0)
        make_identity(nc, identity[:], nomemset=True)

        key_scales = [held.tile([P, HALF // 4], I32, name="key_scales%d" % h, align_bytes=64) for h in range(2)]
        for plane in key_scales:
            nc.vector.memset(plane[:], 0)
        value_scales = held.tile([P, PAGES * DV // 4], I32, name="value_scales", align_bytes=64)
        nc.vector.memset(value_scales[:], 0)

        vs_pool = reused.tile([P, POOL], F32, name="vs_pool", align_bytes=64, offset=VS_AT)
        for h in range(2):
            rows = reused.tile([P, HALF], U8, name="key_scale_rows%d" % h, align_bytes=64, offset=VS_AT + POOL * 4 + h * HALF)
            nc.vector.tensor_copy(
                rows[:], key_scale_pool[:].bitcast(U8).indirect(slot_list[:, h * HALF // 16 : (h + 1) * HALF // 16])
            )
            for r in range(4):
                nc.sync.dma_start(key_scales[h][r:P:32, :], rows[:].bitcast(I32)[ROWS_AT + 4 * r : ROWS_AT + 64 : 16, :])
            if h == 0:
                nc.sync.dma_start(vs_pool[:, : POOL - SPREAD], vs[:, : POOL - SPREAD])

        value_pool = reused.tile([P, POOL_PAGES * DV], I32, name="value_pool", align_bytes=64, offset=0)
        nc.sync.dma_start(
            value_pool[:].rearrange("p (u e) -> p u e", u=POOL_PAGES),
            v_words.rearrange("u p e r -> p u (e r)").bitcast(I32),
        )

        gate_logits = reused.tile([P, DV], F32, name="gate_logits", align_bytes=64, offset=VS_AT + POOL * 4 + HALF)
        nc.sync.dma_start(gate_logits[:], og[0])

        value_scale_rows = held.tile([P, PAGES * DV], U8, name="value_scale_rows")
        nc.vector.tensor_copy(value_scale_rows[:], value_scale_pool[:].bitcast(U8).indirect(column_list[:]))
        for r in range(4):
            nc.sync.dma_start(value_scales[r:P:32, :], value_scale_rows[:].bitcast(I32)[ROWS_AT + 4 * r : ROWS_AT + 64 : 16, :])


        vs_places = vs_pool[:, POOL - SPREAD :].rearrange("m (p h a) -> m h p a", p=P, a=4)
        for h in range(SPREAD // P // 4):
            spread = banks.tile([P, 4, P], F32, name="bank")
            for a in range(4):
                j = 4 * h + a
                nc.tensor.transpose(spread[:, a, :], vs_runs[:, j : j + 1].to_broadcast([P, P]), identity[:])
            nc.scalar.activation(vs_places[:, h], spread[:].rearrange("m a p -> m p a"), ACT.Copy)

        def page_slots(g):
            return slice(g * PAGE, (g + 1) * PAGE)

        key_codes = [
            keys_then_exp.tile([P, PAGE], U32, name="key_codes%d" % g, align_bytes=64, offset=g * PAGE * 4)
            for g in range(PAGES)
        ]
        runs = [(0, PAGE // 2), (PAGE // 2, PAGE // 2)] + [(g * PAGE, PAGE) for g in range(1, PAGES)]
        for first, width in runs:
            nc.vector.tensor_copy(
                key_codes[first // PAGE][:, first % PAGE : first % PAGE + width],
                key_pool[:].bitcast(U32).indirect(slot_list[:, first // 16 : (first + width) // 16]),
            )

        capped = held.tile([P, SLOTS + PAGES - 1], F32, name="capped")

        def score_and_cap(first, width):
            scores = banks.tile([P, width], F32, name="bank")
            nc.tensor.matmul_mx(
                scores[:],
                lhsT=query_codes[:].bitcast(FP8X4),
                lhsT_scale=query_scales[:].bitcast(U8),
                rhs=key_codes[first // PAGE][:, first % PAGE : first % PAGE + width].bitcast(FP8X4),
                rhs_scale=key_scales[first // HALF][:].bitcast(U8)[:, first % HALF : first % HALF + width],
                start=True,
                stop=True,
            )
            nc.scalar.activation(capped[:, first : first + width], scores[:], ACT.Tanh, scale=1.0 / CAP)

        def page_maximum(g):
            nc.vector.tensor_reduce(capped[:, SLOTS + g : SLOTS + g + 1], capped[:, page_slots(g)], AXIS.X, ALU.max)

        exp_neg_max = held.tile([P, 1], F32, name="exp_neg_max")
        first_exp = held.tile([P, PAGE], F32, name="first_exp")
        second_exp = keys_then_exp.tile([P, PAGE], F32, name="second_exp", align_bytes=64, offset=(PAGES - 2) * PAGE * 4)
        later_exp = keys_then_exp.tile([P, HALF], F32, name="later_exp", align_bytes=64, offset=(PAGES - 1) * PAGE * 4)

        def exp_capped(first, width):
            if first < PAGE:
                return first_exp[:, first : first + width]
            if first < HALF:
                return second_exp[:, first - PAGE : first - PAGE + width]
            return later_exp[:, first - HALF : first - HALF + width]

        run_sums = held.tile([P, len(runs)], F32, name="run_sums")

        def exponentials(j):
            first, width = runs[j]
            nc.scalar.activation(
                exp_capped(first, width),
                capped[:, first : first + width],
                ACT.Exp,
                scale=CAP,
                accum_out=run_sums[:, j : j + 1],
            )

        scaled = {}
        grouped = {}
        weights = {}
        codes = {}

        def times_vs(g, parts):
            scaled[g] = stage.tile([P, PAGE], F32, name="scaled%d" % g, align_bytes=64, offset=g * PAGE * 4)
            width = PAGE // parts
            for first in range(0, PAGE, width):
                slot = g * PAGE + first
                nc.vector.tensor_tensor(
                    scaled[g][:, first : first + width],
                    vs_pool[:].indirect(slot_list[:, slot // 16 : (slot + width) // 16]),
                    exp_capped(slot, width),
                    ALU.mult,
                )

        def round_weights(g, halves, on_vector):
            if g not in weights:
                weights[g] = ring.tile([P, 2, P, 2], BF16, name="weights")
            source = scaled[g][:].rearrange("q (s u e) -> q u s e", u=2, e=2)[:, halves]
            if on_vector:
                nc.vector.tensor_scalar(weights[g][:, halves], source, exp_neg_max[:], None, ALU.mult)
            else:
                nc.scalar.activation(weights[g][:, halves], source, ACT.Copy, scale=exp_neg_max[:])

        def turn(g):
            words = weights[g][:].rearrange("q u s e -> q (u s e)").bitcast(F32)
            turned = banks.tile([P, 2, NQ], F32, name="bank")
            for u in range(2):
                nc.tensor.transpose(turned[:, u, :], words[:, u * P : (u + 1) * P], identity[:])
            grouped[g] = stage.tile(
                [P, NQ * 4], BF16, name="grouped%d" % g, align_bytes=64, offset=(PAGES + g) * PAGE * 4
            )
            nc.scalar.copy(
                grouped[g][:].bitcast(F32).rearrange("s (q u) -> s q u", u=2), turned[:].rearrange("s u q -> s q u")
            )

        def quantise(g):
            weight_codes = ring.tile([P, NQ], U32, name="weight_codes", align_bytes=64)
            weight_scales = ring.tile([P, NQ], U8, name="weight_scales", align_bytes=64)
            nc.vector.quantize_mx(out=weight_codes[:].bitcast(FP8X4), scales=weight_scales[:], in_=grouped[g][:])
            codes[g] = (weight_codes, weight_scales)

        score_and_cap(*runs[0])
        score_and_cap(*runs[1])
        page_maximum(0)
        exponentials(0)
        exponentials(1)
        times_vs(0, 1)
        score_and_cap(*runs[2])
        page_maximum(1)
        score_and_cap(*runs[3])
        page_maximum(2)
        exponentials(2)
        times_vs(1, 1)
        score_and_cap(*runs[4])
        row_max = stage.tile([P, 1], F32, name="row_max", align_bytes=64, offset=(PAGES - 1) * PAGE * 4)
        nc.vector.tensor_reduce(row_max[:], capped[:, (PAGES - 1) * PAGE :], AXIS.X, ALU.max)
        exponentials(3)
        times_vs(2, 1)
        exponentials(4)
        nc.scalar.activation(exp_neg_max[:], row_max[:], ACT.Exp, scale=-CAP)
        gate_tanh = capped[:, HALF : HALF + DV]
        nc.scalar.activation(gate_tanh, gate_logits[:], ACT.Tanh, scale=0.5)
        low, high, both = slice(0, 1), slice(1, 2), slice(0, 2)
        round_weights(0, low, True)
        round_weights(0, high, False)
        times_vs(3, 1)
        for half in (low, high):
            round_weights(1, half, False)
        for g in range(2, PAGES):
            round_weights(g, both, True)
        for g in range(PAGES):
            turn(g)

        gate = held.tile([P, DV], F32, name="gate")
        nc.scalar.activation(gate[:], gate_tanh, ACT.Copy, scale=0.5, bias=0.5)

        value_codes = reused.tile([P, PAGES * DV], U32, name="value_codes", align_bytes=64, offset=VS_AT)
        nc.vector.tensor_copy(value_codes[:], value_pool[:].bitcast(U32).indirect(column_list[:]))
        for g in range(PAGES):
            quantise(g)

        scaled_sums = held.tile([P, len(runs)], F32, name="scaled_sums")
        row_sum = held.tile([P, 1], F32, name="row_sum")
        nc.scalar.activation(scaled_sums[:], run_sums[:], ACT.Copy, scale=exp_neg_max[:], accum_out=row_sum[:])
        inverse_sum = reused.tile([P, 1], F32, name="inverse_sum", align_bytes=64, offset=VS_AT + PAGES * DV * 5)
        nc.vector.reciprocal(inverse_sum[:], row_sum[:])

        sums = out_bank.tile([P, DV], F32, name="sums")
        for g in range(PAGES):
            columns = slice(g * DV, (g + 1) * DV)
            nc.tensor.matmul_mx(
                sums[:],
                lhsT=codes[g][0][:].bitcast(FP8X4),
                lhsT_scale=codes[g][1][:],
                rhs=value_codes[:, columns].bitcast(FP8X4),
                rhs_scale=value_scales[:].bitcast(U8)[:, columns],
                start=(g == 0),
                stop=(g == PAGES - 1),
            )

        result = held.tile([P, DV], F32, name="result")
        nc.vector.scalar_tensor_tensor(result[:], sums[:], inverse_sum[:], gate[:], ALU.mult, ALU.mult)
        nc.sync.dma_start(out[0], result[:])
